import numpy as np
import ml_dtypes


def mxq(x, axis, fmt="e4m3"):
    dtype, down = {"e4m3": (ml_dtypes.float8_e4m3fn, 7), "e5m2": (ml_dtypes.float8_e5m2, 14)}[fmt]
    v = np.moveaxis(np.asarray(x, np.float32).astype(ml_dtypes.bfloat16).astype(np.float64), axis, -1)
    blocks = v.reshape(v.shape[:-1] + (-1, 32))
    amax = np.abs(blocks).max(-1, keepdims=True)
    byte = np.maximum(np.where(amax > 0, np.frexp(amax)[1] - 1 + 127, 0) - down, 1)
    scale = np.exp2(byte - 127.0)
    codes = (blocks / scale).astype(np.float32).astype(dtype).astype(np.float64)
    return np.moveaxis((codes * scale).reshape(v.shape), -1, axis)


WIDE = False


def mx_kscale(k):
    if not WIDE:
        return np.ones(k)
    levels = np.array([10, -10, 5, -5, 0])
    if k % 512:
        return np.exp2(np.random.permutation(np.resize(levels, k // 32))).repeat(32)
    a = np.empty((k // 512, 16))
    for p in range(k // 512):
        a[p, :8] = np.random.permutation(np.resize(levels, 8))
        for g in range(8):
            far = levels[np.abs(levels - a[p, g]) >= 10]
            a[p, g + 8] = far[np.random.randint(len(far))]
    return np.exp2(a.ravel()).repeat(32)


def f64(x):
    return np.asarray(x).astype(np.float64)


def striped(idx):
    return np.tile(idx.reshape(-1, 16).T, (8, 1)).astype(np.uint16)


def unstriped(offs):
    return offs[:16].T.reshape(-1).astype(np.int64)


def relu(v):
    return np.maximum(v, 0.0)


K, T, S, V, N = 512, 4096, 1024, 512, 256


def setup_inputs():
    n = np.random.standard_normal
    s = mx_kscale(K)[:, None]
    return {
        "xT": (n((K, T)) * s).astype(np.float32),
        "sT": (n((K, V)) * s).astype(np.float32),
        "w1": (n((K, N)) / np.sqrt(K) / s).astype(np.float32),
        "w2": (n((K, N)) / np.sqrt(K) / s).astype(np.float32),
        "offs": striped(np.random.permutation(T)[:S]),
        "par": striped(np.random.randint(0, V, S)),
    }


def reference(xT, sT, w1, w2, offs, par):
    xq = mxq(f64(xT)[:, unstriped(offs)], 0, "e4m3")
    y = mxq(f64(w1), 0, "e4m3").T @ xq
    t = mxq(f64(w2), 0, "e4m3").T @ mxq(f64(sT), 0, "e4m3")
    return relu(y + t[:, unstriped(par)])

@@ -1,0 +1,100 @@
+from contextlib import ExitStack
+
+import concourse.mybir as mybir
+
+K, T, S, V, N = 512, 4096, 1024, 512, 256
+FLOPS = 2 * K * N * (S + V)
+
+F32 = mybir.dt.float32
+BF16 = mybir.dt.bfloat16
+U32 = mybir.dt.uint32
+U16 = mybir.dt.uint16
+U8 = mybir.dt.uint8
+FP8X4 = mybir.dt.float8_e4m3fn_x4
+ADD = mybir.AluOpType.add
+RELU = mybir.ActivationFunctionType.Relu
+
+P = 128
+PACK = 4
+HALF = S // 2
+LIST_ROWS = 16
+PAR_PIECE = V // 2
+
+
+def tile_picked_fpn_relu_e_kernel(tc, xT, sT, w1, w2, offs, par, out):
+    nc = tc.nc
+    with ExitStack() as ctx:
+        lists = ctx.enter_context(tc.tile_pool(name="lists", bufs=1))
+        sb = ctx.enter_context(tc.tile_pool(name="sb", bufs=1))
+        psum = ctx.enter_context(tc.psum_pool(name="psum", bufs=1))
+
+        def load_rows(src, name):
+            raw = sb.tile([P, PACK, src.shape[1]], F32, name=name + "_raw")
+            nc.sync.dma_start(out=raw[:], in_=src.rearrange("(p j) c -> p j c", j=PACK))
+            return raw
+
+        def interleave(copy, raw, name):
+            grouped = sb.tile([P, raw.shape[2], PACK], BF16, name=name + "_bf", align_bytes=64)
+            copy(out=grouped[:].rearrange("p (c i) j -> p c j i", i=4), in_=raw[:].rearrange("p j (c i) -> p c j i", i=4))
+            return grouped
+
+        def quantize(grouped, name):
+            width = grouped.shape[1]
+            codes = sb.tile([P, width], U32, name=name + "_codes", align_bytes=64)
+            scales = sb.tile([P, width], U8, name=name + "_scales", align_bytes=64)
+            nc.vector.quantize_mx(out=codes[:].bitcast(FP8X4), scales=scales[:], in_=grouped[:].rearrange("p c j -> p (c j)"))
+            return codes, scales
+
+        def product(weights, m, cells, name):
+            acc = psum.tile([P, cells[0].shape[1]], F32, name=name)
+            rows = slice(m * P, (m + 1) * P)
+            nc.tensor.matmul_mx(out=acc[:], lhsT=weights[0][:, rows].bitcast(FP8X4), lhsT_scale=weights[1][:, rows],
+                                rhs=cells[0][:].bitcast(FP8X4), rhs_scale=cells[1][:], start=True, stop=True)
+            return acc
+
+        def entries(lst, first, count):
+            return lst[:, first // LIST_ROWS : (first + count) // LIST_ROWS]
+
+        s_raw = load_rows(sT, "s")
+        w2_raw = load_rows(w2, "w2")
+        par_sb = lists.tile([P, S // LIST_ROWS], U16, name="par_sb")
+        nc.sync.dma_start(par_sb[:], par)
+        offs_sb = lists.tile([P, S // LIST_ROWS], U16, name="offs_sb")
+        nc.sync.dma_start(offs_sb[:], offs)
+        x_rows = xT.rearrange("(p j) t -> p j t", j=PACK)
+        x_plane = [sb.tile([P, T], F32, name="x_plane%d" % j) for j in range(PACK)]
+        for j in range(2):
+            nc.sync.dma_start(out=x_plane[j][:], in_=x_rows[:, j, :])
+        w1_raw = load_rows(w1, "w1")
+        for j in range(2, PACK):
+            nc.sync.dma_start(out=x_plane[j][:], in_=x_rows[:, j, :])
+
+        s_q = quantize(interleave(nc.vector.tensor_copy, s_raw, "s"), "s")
+        w2_q = quantize(interleave(nc.scalar.copy, w2_raw, "w2"), "w2")
+        parent = {}
+        for m in range(N // P):
+            t_ps = product(w2_q, m, s_q, "t_ps%d" % m)
+            t_sb = sb.tile([P, V], F32, name="t_sb%d" % m)
+            nc.scalar.copy(out=t_sb[:], in_=t_ps[:])
+            for h in range(2):
+                parent[m, h] = sb.tile([P, HALF], F32, name="parent%d%d" % (m, h))
+                for c in range(0, HALF, PAR_PIECE):
+                    nc.vector.tensor_copy(out=parent[m, h][:, c : c + PAR_PIECE],
+                                          in_=t_sb[:].indirect(entries(par_sb, h * HALF + c, PAR_PIECE)))
+
+        picked = [sb.tile([P, HALF, PACK], BF16, name="picked%d" % h, align_bytes=64) for h in range(2)]
+        for j in range(PACK):
+            for h in range(2):
+                nc.vector.tensor_copy(out=picked[h][:, :, j], in_=x_plane[j][:].indirect(entries(offs_sb, h * HALF, HALF)))
+            if j == 1:
+                w1_q = quantize(interleave(nc.scalar.copy, w1_raw, "w1"), "w1")
+
+        x_q = [quantize(picked[h], "x%d" % h) for h in range(2)]
+        for h in range(2):
+            for m in range(N // P):
+                y_ps = product(w1_q, m, x_q[h], "y_ps%d%d" % (m, h))
+                total = sb.tile([P, HALF], F32, name="total%d%d" % (m, h))
+                nc.vector.tensor_tensor(out=total[:], in0=y_ps[:], in1=parent[m, h][:], op=ADD)
+                result = sb.tile([P, HALF], F32, name="result%d%d" % (m, h))
+                nc.scalar.activation(out=result[:], in_=total[:], func=RELU)
+                nc.sync.dma_start(out=out[m * P : (m + 1) * P, h * HALF : (h + 1) * HALF], in_=result[:])

@@ -12,6 +12,7 @@ U16 = mybir.dt.uint16
 U8 = mybir.dt.uint8
 FP8X4 = mybir.dt.float8_e4m3fn_x4
 ADD = mybir.AluOpType.add
+COPY = mybir.ActivationFunctionType.Copy
 RELU = mybir.ActivationFunctionType.Relu
 
 P = 128
@@ -19,6 +20,7 @@ PACK = 4
 HALF = S // 2
 LIST_ROWS = 16
 PAR_PIECE = V // 2
+LAST_CUTS = (0, 1024, 2048, 2816, 3584, 4096)
 
 
 def tile_picked_fpn_relu_e_kernel(tc, xT, sT, w1, w2, offs, par, out):
@@ -35,7 +37,7 @@ def tile_picked_fpn_relu_e_kernel(tc, xT, sT, w1, w2, offs, par, out):
 
         def interleave(copy, raw, name):
             grouped = sb.tile([P, raw.shape[2], PACK], BF16, name=name + "_bf", align_bytes=64)
-            copy(out=grouped[:].rearrange("p (c i) j -> p c j i", i=4), in_=raw[:].rearrange("p j (c i) -> p c j i", i=4))
+            copy(out=grouped[:].rearrange("p (c i) j -> p c j i", i=4), in_=raw.rearrange("p j (c i) -> p c j i", i=4))
             return grouped
 
         def quantize(grouped, name):
@@ -45,9 +47,8 @@ def tile_picked_fpn_relu_e_kernel(tc, xT, sT, w1, w2, offs, par, out):
             nc.vector.quantize_mx(out=codes[:].bitcast(FP8X4), scales=scales[:], in_=grouped[:].rearrange("p c j -> p (c j)"))
             return codes, scales
 
-        def product(weights, m, cells, name):
+        def product(weights, rows, cells, name):
             acc = psum.tile([P, cells[0].shape[1]], F32, name=name)
-            rows = slice(m * P, (m + 1) * P)
             nc.tensor.matmul_mx(out=acc[:], lhsT=weights[0][:, rows].bitcast(FP8X4), lhsT_scale=weights[1][:, rows],
                                 rhs=cells[0][:].bitcast(FP8X4), rhs_scale=cells[1][:], start=True, stop=True)
             return acc
@@ -57,42 +58,58 @@ def tile_picked_fpn_relu_e_kernel(tc, xT, sT, w1, w2, offs, par, out):
 
         s_raw = load_rows(sT, "s")
         w2_raw = load_rows(w2, "w2")
+        w1_raw = load_rows(w1, "w1")
         par_sb = lists.tile([P, S // LIST_ROWS], U16, name="par_sb")
         nc.sync.dma_start(par_sb[:], par)
         offs_sb = lists.tile([P, S // LIST_ROWS], U16, name="offs_sb")
         nc.sync.dma_start(offs_sb[:], offs)
         x_rows = xT.rearrange("(p j) t -> p j t", j=PACK)
         x_plane = [sb.tile([P, T], F32, name="x_plane%d" % j) for j in range(PACK)]
-        for j in range(2):
+        for j in (2, 0, 1):
             nc.sync.dma_start(out=x_plane[j][:], in_=x_rows[:, j, :])
-        w1_raw = load_rows(w1, "w1")
-        for j in range(2, PACK):
-            nc.sync.dma_start(out=x_plane[j][:], in_=x_rows[:, j, :])
+        for first, end in zip(LAST_CUTS, LAST_CUTS[1:]):
+            nc.sync.dma_start(out=x_plane[3][:, first:end], in_=x_rows[:, 3, first:end])
 
-        s_q = quantize(interleave(nc.vector.tensor_copy, s_raw, "s"), "s")
-        w2_q = quantize(interleave(nc.scalar.copy, w2_raw, "w2"), "w2")
-        parent = {}
+        s_q = quantize(interleave(nc.vector.tensor_copy, s_raw[:], "s"), "s")
+        t_sb = []
         for m in range(N // P):
-            t_ps = product(w2_q, m, s_q, "t_ps%d" % m)
-            t_sb = sb.tile([P, V], F32, name="t_sb%d" % m)
-            nc.scalar.copy(out=t_sb[:], in_=t_ps[:])
+            w2_q = quantize(interleave(nc.scalar.copy, w2_raw[:, :, m * P : (m + 1) * P], "w2_%d" % m), "w2_%d" % m)
+            t_ps = product(w2_q, slice(0, P), s_q, "t_ps%d" % m)
+            t_sb.append(sb.tile([P, V], F32, name="t_sb%d" % m))
+            nc.scalar.copy(out=t_sb[m][:], in_=t_ps[:])
+
+        w1_q = quantize(interleave(nc.scalar.copy, w1_raw[:], "w1"), "w1")
+        parent = {}
+
+        def fetch_parents(m):
             for h in range(2):
                 parent[m, h] = sb.tile([P, HALF], F32, name="parent%d%d" % (m, h))
                 for c in range(0, HALF, PAR_PIECE):
                     nc.vector.tensor_copy(out=parent[m, h][:, c : c + PAR_PIECE],
-                                          in_=t_sb[:].indirect(entries(par_sb, h * HALF + c, PAR_PIECE)))
+                                          in_=t_sb[m][:].indirect(entries(par_sb, h * HALF + c, PAR_PIECE)))
 
+        fetch_parents(0)
         picked = [sb.tile([P, HALF, PACK], BF16, name="picked%d" % h, align_bytes=64) for h in range(2)]
-        for j in range(PACK):
-            for h in range(2):
+        dense = sb.tile([P, HALF], BF16, name="dense")
+        nc.vector.tensor_copy(out=dense[:], in_=x_plane[2][:].indirect(entries(offs_sb, HALF, HALF)))
+        nc.scalar.copy(out=picked[1][:, :, 2], in_=dense[:])
+        nc.vector.tensor_copy(out=picked[0][:, :, 2], in_=x_plane[2][:].indirect(entries(offs_sb, 0, HALF)))
+        fetch_parents(1)
+
+        for j in (0, 1):
+            for h in (1, 0):
                 nc.vector.tensor_copy(out=picked[h][:, :, j], in_=x_plane[j][:].indirect(entries(offs_sb, h * HALF, HALF)))
-            if j == 1:
-                w1_q = quantize(interleave(nc.scalar.copy, w1_raw, "w1"), "w1")
+        last_bf = sb.tile([P, T], BF16, name="last_bf")
+        for i, (first, end) in enumerate(zip(LAST_CUTS, LAST_CUTS[1:])):
+            copy = nc.vector.tensor_copy if i == 3 else nc.scalar.copy
+            copy(out=last_bf[:, first:end], in_=x_plane[3][:, first:end])
+        nc.vector.tensor_copy(out=picked[0][:, :, 3], in_=x_plane[3][:].indirect(entries(offs_sb, 0, HALF)))
+        nc.scalar.activation(out=picked[1][:, :, 3], in_=last_bf[:].indirect(entries(offs_sb, HALF, HALF)), func=COPY)
 
         x_q = [quantize(picked[h], "x%d" % h) for h in range(2)]
         for h in range(2):
             for m in range(N // P):
-                y_ps = product(w1_q, m, x_q[h], "y_ps%d%d" % (m, h))
+                y_ps = product(w1_q, slice(m * P, (m + 1) * P), x_q[h], "y_ps%d%d" % (m, h))
                 total = sb.tile([P, HALF], F32, name="total%d%d" % (m, h))
                 nc.vector.tensor_tensor(out=total[:], in0=y_ps[:], in1=parent[m, h][:], op=ADD)
                 result = sb.tile([P, HALF], F32, name="result%d%d" % (m, h))

@@ -20,6 +20,7 @@ PACK = 4
 HALF = S // 2
 LIST_ROWS = 16
 PAR_PIECE = V // 2
+QUARTER = S // 4
 LAST_CUTS = (0, 1024, 2048, 2816, 3584, 4096)
 
 
@@ -38,20 +39,18 @@ def tile_picked_fpn_relu_e_kernel(tc, xT, sT, w1, w2, offs, par, out):
         def interleave(copy, raw, name):
             grouped = sb.tile([P, raw.shape[2], PACK], BF16, name=name + "_bf", align_bytes=64)
             copy(out=grouped[:].rearrange("p (c i) j -> p c j i", i=4), in_=raw.rearrange("p j (c i) -> p c j i", i=4))
-            return grouped
+            return grouped[:]
 
         def quantize(grouped, name):
             width = grouped.shape[1]
             codes = sb.tile([P, width], U32, name=name + "_codes", align_bytes=64)
             scales = sb.tile([P, width], U8, name=name + "_scales", align_bytes=64)
-            nc.vector.quantize_mx(out=codes[:].bitcast(FP8X4), scales=scales[:], in_=grouped[:].rearrange("p c j -> p (c j)"))
+            nc.vector.quantize_mx(out=codes[:].bitcast(FP8X4), scales=scales[:], in_=grouped.rearrange("p c j -> p (c j)"))
             return codes, scales
 
-        def product(weights, rows, cells, name):
-            acc = psum.tile([P, cells[0].shape[1]], F32, name=name)
-            nc.tensor.matmul_mx(out=acc[:], lhsT=weights[0][:, rows].bitcast(FP8X4), lhsT_scale=weights[1][:, rows],
-                                rhs=cells[0][:].bitcast(FP8X4), rhs_scale=cells[1][:], start=True, stop=True)
-            return acc
+        def multiply(acc, weights, rows, cells, cols):
+            nc.tensor.matmul_mx(out=acc, lhsT=weights[0][:, rows].bitcast(FP8X4), lhsT_scale=weights[1][:, rows],
+                                rhs=cells[0][:, cols].bitcast(FP8X4), rhs_scale=cells[1][:, cols], start=True, stop=True)
 
         def entries(lst, first, count):
             return lst[:, first // LIST_ROWS : (first + count) // LIST_ROWS]
@@ -74,7 +73,8 @@ def tile_picked_fpn_relu_e_kernel(tc, xT, sT, w1, w2, offs, par, out):
         t_sb = []
         for m in range(N // P):
             w2_q = quantize(interleave(nc.scalar.copy, w2_raw[:, :, m * P : (m + 1) * P], "w2_%d" % m), "w2_%d" % m)
-            t_ps = product(w2_q, slice(0, P), s_q, "t_ps%d" % m)
+            t_ps = psum.tile([P, V], F32, name="t_ps%d" % m)
+            multiply(t_ps[:], w2_q, slice(0, P), s_q, slice(0, V))
             t_sb.append(sb.tile([P, V], F32, name="t_sb%d" % m))
             nc.scalar.copy(out=t_sb[m][:], in_=t_ps[:])
 
@@ -99,19 +99,46 @@ def tile_picked_fpn_relu_e_kernel(tc, xT, sT, w1, w2, offs, par, out):
         for j in (0, 1):
             for h in (1, 0):
                 nc.vector.tensor_copy(out=picked[h][:, :, j], in_=x_plane[j][:].indirect(entries(offs_sb, h * HALF, HALF)))
-        last_bf = sb.tile([P, T], BF16, name="last_bf")
+        last_bf = sb.tile([P, T], BF16, name="last_bf", tag="last_bf")
         for i, (first, end) in enumerate(zip(LAST_CUTS, LAST_CUTS[1:])):
             copy = nc.vector.tensor_copy if i == 3 else nc.scalar.copy
             copy(out=last_bf[:, first:end], in_=x_plane[3][:, first:end])
         nc.vector.tensor_copy(out=picked[0][:, :, 3], in_=x_plane[3][:].indirect(entries(offs_sb, 0, HALF)))
         nc.scalar.activation(out=picked[1][:, :, 3], in_=last_bf[:].indirect(entries(offs_sb, HALF, HALF)), func=COPY)
 
-        x_q = [quantize(picked[h], "x%d" % h) for h in range(2)]
-        for h in range(2):
-            for m in range(N // P):
-                y_ps = product(w1_q, slice(m * P, (m + 1) * P), x_q[h], "y_ps%d%d" % (m, h))
-                total = sb.tile([P, HALF], F32, name="total%d%d" % (m, h))
-                nc.vector.tensor_tensor(out=total[:], in0=y_ps[:], in1=parent[m, h][:], op=ADD)
-                result = sb.tile([P, HALF], F32, name="result%d%d" % (m, h))
-                nc.scalar.activation(out=result[:], in_=total[:], func=RELU)
-                nc.sync.dma_start(out=out[m * P : (m + 1) * P, h * HALF : (h + 1) * HALF], in_=result[:])
+        w1_rows = [slice(m * P, (m + 1) * P) for m in range(N // P)]
+        first_q = [quantize(picked[0][:, c : c + QUARTER, :], "x0_%d" % c) for c in (0, QUARTER)]
+        second_q = quantize(picked[1][:], "x1")
+
+        totals = sb.tile([P, N // P, S], F32, name="totals", tag="last_bf")
+
+        def finish(acc, m, first, relu, queue):
+            width = acc.shape[1]
+            h, c = divmod(first, HALF)
+            total = totals[:, m, first : first + width]
+            nc.vector.tensor_tensor(out=total, in0=acc, in1=parent[m, h][:, c : c + width], op=ADD)
+            result = sb.tile([P, width], F32, name="result%d_%d" % (m, first))
+            relu(result[:], total)
+            queue.dma_start(out=out[w1_rows[m], first : first + width], in_=result[:])
+
+        def scalar_relu(result, total):
+            nc.scalar.activation(out=result, in_=total, func=RELU)
+
+        def vector_relu(result, total):
+            nc.vector.tensor_scalar_max(out=result, in0=total, scalar1=0.0)
+
+        for i in range(2):
+            acc = psum.tile([P, QUARTER], F32, name="y_first0_%d" % i)
+            multiply(acc[:], w1_q, w1_rows[0], first_q[i], slice(0, QUARTER))
+            finish(acc[:], 0, i * QUARTER, scalar_relu, nc.sync)
+        acc = psum.tile([P, HALF], F32, name="y_first1")
+        for i in range(2):
+            multiply(acc[:, i * QUARTER : (i + 1) * QUARTER], w1_q, w1_rows[1], first_q[i], slice(0, QUARTER))
+        finish(acc[:], 1, 0, scalar_relu, nc.sync)
+        acc = psum.tile([P, HALF], F32, name="y_second0")
+        multiply(acc[:], w1_q, w1_rows[0], second_q, slice(0, HALF))
+        finish(acc[:], 0, HALF, scalar_relu, nc.sync)
+        for i, (relu, queue) in enumerate(((vector_relu, nc.sync), (scalar_relu, nc.sync))):
+            acc = psum.tile([P, QUARTER], F32, name="y_second1_%d" % i)
+            multiply(acc[:], w1_q, w1_rows[1], second_q, slice(i * QUARTER, (i + 1) * QUARTER))
+            finish(acc[:], 1, HALF + i * QUARTER, relu, queue)

@@ -90,9 +90,9 @@ def tile_picked_fpn_relu_e_kernel(tc, xT, sT, w1, w2, offs, par, out):
 
         fetch_parents(0)
         picked = [sb.tile([P, HALF, PACK], BF16, name="picked%d" % h, align_bytes=64) for h in range(2)]
-        dense = sb.tile([P, HALF], BF16, name="dense")
-        nc.vector.tensor_copy(out=dense[:], in_=x_plane[2][:].indirect(entries(offs_sb, HALF, HALF)))
-        nc.scalar.copy(out=picked[1][:, :, 2], in_=dense[:])
+        first_bf = sb.tile([P, T], BF16, name="first_bf")
+        nc.scalar.copy(out=first_bf[:], in_=x_plane[2][:])
+        nc.scalar.activation(out=picked[1][:, :, 2], in_=first_bf[:].indirect(entries(offs_sb, HALF, HALF)), func=COPY)
         nc.vector.tensor_copy(out=picked[0][:, :, 2], in_=x_plane[2][:].indirect(entries(offs_sb, 0, HALF)))
         fetch_parents(1)
 
@@ -134,10 +134,12 @@ def tile_picked_fpn_relu_e_kernel(tc, xT, sT, w1, w2, offs, par, out):
         acc = psum.tile([P, HALF], F32, name="y_first1")
         for i in range(2):
             multiply(acc[:, i * QUARTER : (i + 1) * QUARTER], w1_q, w1_rows[1], first_q[i], slice(0, QUARTER))
-        finish(acc[:], 1, 0, scalar_relu, nc.sync)
+        for c in (0, QUARTER):
+            finish(acc[:, c : c + QUARTER], 1, c, scalar_relu, nc.sync)
         acc = psum.tile([P, HALF], F32, name="y_second0")
         multiply(acc[:], w1_q, w1_rows[0], second_q, slice(0, HALF))
-        finish(acc[:], 0, HALF, scalar_relu, nc.sync)
+        for c in (0, QUARTER):
+            finish(acc[:, c : c + QUARTER], 0, HALF + c, scalar_relu, nc.sync)
         for i, (relu, queue) in enumerate(((vector_relu, nc.sync), (scalar_relu, nc.sync))):
             acc = psum.tile([P, QUARTER], F32, name="y_second1_%d" % i)
             multiply(acc[:], w1_q, w1_rows[1], second_q, slice(i * QUARTER, (i + 1) * QUARTER))

@@ -17,11 +17,15 @@ RELU = mybir.ActivationFunctionType.Relu
 
 P = 128
 PACK = 4
-HALF = S // 2
 LIST_ROWS = 16
-PAR_PIECE = V // 2
+HALF = S // 2
 QUARTER = S // 4
+PAR_PIECE = V // 2
+RUN = 4
+
+FIRST_PLANE, MIDDLE_PLANES, LAST_PLANE = 2, (0, 1), 3
 LAST_CUTS = (0, 1024, 2048, 2816, 3584, 4096)
+VECTOR_PIECE = 3
 
 
 def tile_picked_fpn_relu_e_kernel(tc, xT, sT, w1, w2, offs, par, out):
@@ -38,22 +42,34 @@ def tile_picked_fpn_relu_e_kernel(tc, xT, sT, w1, w2, offs, par, out):
 
         def interleave(copy, raw, name):
             grouped = sb.tile([P, raw.shape[2], PACK], BF16, name=name + "_bf", align_bytes=64)
-            copy(out=grouped[:].rearrange("p (c i) j -> p c j i", i=4), in_=raw.rearrange("p j (c i) -> p c j i", i=4))
+            copy(
+                out=grouped[:].rearrange("p (c i) j -> p c j i", i=RUN),
+                in_=raw.rearrange("p j (c i) -> p c j i", i=RUN),
+            )
             return grouped[:]
 
         def quantize(grouped, name):
             width = grouped.shape[1]
             codes = sb.tile([P, width], U32, name=name + "_codes", align_bytes=64)
             scales = sb.tile([P, width], U8, name=name + "_scales", align_bytes=64)
-            nc.vector.quantize_mx(out=codes[:].bitcast(FP8X4), scales=scales[:], in_=grouped.rearrange("p c j -> p (c j)"))
+            nc.vector.quantize_mx(
+                out=codes[:].bitcast(FP8X4), scales=scales[:], in_=grouped.rearrange("p c j -> p (c j)")
+            )
             return codes, scales
 
         def multiply(acc, weights, rows, cells, cols):
-            nc.tensor.matmul_mx(out=acc, lhsT=weights[0][:, rows].bitcast(FP8X4), lhsT_scale=weights[1][:, rows],
-                                rhs=cells[0][:, cols].bitcast(FP8X4), rhs_scale=cells[1][:, cols], start=True, stop=True)
+            nc.tensor.matmul_mx(
+                out=acc,
+                lhsT=weights[0][:, rows].bitcast(FP8X4),
+                lhsT_scale=weights[1][:, rows],
+                rhs=cells[0][:, cols].bitcast(FP8X4),
+                rhs_scale=cells[1][:, cols],
+                start=True,
+                stop=True,
+            )
 
-        def entries(lst, first, count):
-            return lst[:, first // LIST_ROWS : (first + count) // LIST_ROWS]
+        def entries(list_tile, first, count):
+            return list_tile[:, first // LIST_ROWS : (first + count) // LIST_ROWS]
 
         s_raw = load_rows(sT, "s")
         w2_raw = load_rows(w2, "w2")
@@ -64,62 +80,68 @@ def tile_picked_fpn_relu_e_kernel(tc, xT, sT, w1, w2, offs, par, out):
         nc.sync.dma_start(offs_sb[:], offs)
         x_rows = xT.rearrange("(p j) t -> p j t", j=PACK)
         x_plane = [sb.tile([P, T], F32, name="x_plane%d" % j) for j in range(PACK)]
-        for j in (2, 0, 1):
+        for j in (FIRST_PLANE, *MIDDLE_PLANES):
             nc.sync.dma_start(out=x_plane[j][:], in_=x_rows[:, j, :])
-        for first, end in zip(LAST_CUTS, LAST_CUTS[1:]):
-            nc.sync.dma_start(out=x_plane[3][:, first:end], in_=x_rows[:, 3, first:end])
+        last_pieces = [slice(first, end) for first, end in zip(LAST_CUTS, LAST_CUTS[1:])]
+        for cols in last_pieces:
+            nc.sync.dma_start(out=x_plane[LAST_PLANE][:, cols], in_=x_rows[:, LAST_PLANE, cols])
 
+        out_rows = [slice(m * P, (m + 1) * P) for m in range(N // P)]
         s_q = quantize(interleave(nc.vector.tensor_copy, s_raw[:], "s"), "s")
         t_sb = []
-        for m in range(N // P):
-            w2_q = quantize(interleave(nc.scalar.copy, w2_raw[:, :, m * P : (m + 1) * P], "w2_%d" % m), "w2_%d" % m)
+        for m, rows in enumerate(out_rows):
+            w2_q = quantize(interleave(nc.scalar.copy, w2_raw[:, :, rows], "w2_%d" % m), "w2_%d" % m)
             t_ps = psum.tile([P, V], F32, name="t_ps%d" % m)
             multiply(t_ps[:], w2_q, slice(0, P), s_q, slice(0, V))
             t_sb.append(sb.tile([P, V], F32, name="t_sb%d" % m))
             nc.scalar.copy(out=t_sb[m][:], in_=t_ps[:])
 
         w1_q = quantize(interleave(nc.scalar.copy, w1_raw[:], "w1"), "w1")
+
         parent = {}
 
         def fetch_parents(m):
             for h in range(2):
                 parent[m, h] = sb.tile([P, HALF], F32, name="parent%d%d" % (m, h))
                 for c in range(0, HALF, PAR_PIECE):
-                    nc.vector.tensor_copy(out=parent[m, h][:, c : c + PAR_PIECE],
-                                          in_=t_sb[m][:].indirect(entries(par_sb, h * HALF + c, PAR_PIECE)))
+                    nc.vector.tensor_copy(
+                        out=parent[m, h][:, c : c + PAR_PIECE],
+                        in_=t_sb[m][:].indirect(entries(par_sb, h * HALF + c, PAR_PIECE)),
+                    )
+
+        def gather_on_vector(j, h):
+            nc.vector.tensor_copy(
+                out=picked[h][:, :, j], in_=x_plane[j][:].indirect(entries(offs_sb, h * HALF, HALF))
+            )
+
+        def gather_on_scalar(j, plane_bf):
+            nc.scalar.activation(
+                out=picked[1][:, :, j], in_=plane_bf[:].indirect(entries(offs_sb, HALF, HALF)), func=COPY
+            )
 
         fetch_parents(0)
         picked = [sb.tile([P, HALF, PACK], BF16, name="picked%d" % h, align_bytes=64) for h in range(2)]
         first_bf = sb.tile([P, T], BF16, name="first_bf")
-        nc.scalar.copy(out=first_bf[:], in_=x_plane[2][:])
-        nc.scalar.activation(out=picked[1][:, :, 2], in_=first_bf[:].indirect(entries(offs_sb, HALF, HALF)), func=COPY)
-        nc.vector.tensor_copy(out=picked[0][:, :, 2], in_=x_plane[2][:].indirect(entries(offs_sb, 0, HALF)))
+        nc.scalar.copy(out=first_bf[:], in_=x_plane[FIRST_PLANE][:])
+        gather_on_scalar(FIRST_PLANE, first_bf)
+        gather_on_vector(FIRST_PLANE, 0)
         fetch_parents(1)
 
-        for j in (0, 1):
+        for j in MIDDLE_PLANES:
             for h in (1, 0):
-                nc.vector.tensor_copy(out=picked[h][:, :, j], in_=x_plane[j][:].indirect(entries(offs_sb, h * HALF, HALF)))
-        last_bf = sb.tile([P, T], BF16, name="last_bf", tag="last_bf")
-        for i, (first, end) in enumerate(zip(LAST_CUTS, LAST_CUTS[1:])):
-            copy = nc.vector.tensor_copy if i == 3 else nc.scalar.copy
-            copy(out=last_bf[:, first:end], in_=x_plane[3][:, first:end])
-        nc.vector.tensor_copy(out=picked[0][:, :, 3], in_=x_plane[3][:].indirect(entries(offs_sb, 0, HALF)))
-        nc.scalar.activation(out=picked[1][:, :, 3], in_=last_bf[:].indirect(entries(offs_sb, HALF, HALF)), func=COPY)
+                gather_on_vector(j, h)
 
-        w1_rows = [slice(m * P, (m + 1) * P) for m in range(N // P)]
+        last_bf = sb.tile([P, T], BF16, name="last_bf", tag="last_bf")
+        for i, cols in enumerate(last_pieces):
+            copy = nc.vector.tensor_copy if i == VECTOR_PIECE else nc.scalar.copy
+            copy(out=last_bf[:, cols], in_=x_plane[LAST_PLANE][:, cols])
+        gather_on_vector(LAST_PLANE, 0)
+        gather_on_scalar(LAST_PLANE, last_bf)
+
         first_q = [quantize(picked[0][:, c : c + QUARTER, :], "x0_%d" % c) for c in (0, QUARTER)]
         second_q = quantize(picked[1][:], "x1")
 
         totals = sb.tile([P, N // P, S], F32, name="totals", tag="last_bf")
-
-        def finish(acc, m, first, relu, queue):
-            width = acc.shape[1]
-            h, c = divmod(first, HALF)
-            total = totals[:, m, first : first + width]
-            nc.vector.tensor_tensor(out=total, in0=acc, in1=parent[m, h][:, c : c + width], op=ADD)
-            result = sb.tile([P, width], F32, name="result%d_%d" % (m, first))
-            relu(result[:], total)
-            queue.dma_start(out=out[w1_rows[m], first : first + width], in_=result[:])
 
         def scalar_relu(result, total):
             nc.scalar.activation(out=result, in_=total, func=RELU)
@@ -127,20 +149,28 @@ def tile_picked_fpn_relu_e_kernel(tc, xT, sT, w1, w2, offs, par, out):
         def vector_relu(result, total):
             nc.vector.tensor_scalar_max(out=result, in0=total, scalar1=0.0)
 
+        def finish(acc, m, first, relu):
+            h, c = divmod(first, HALF)
+            total = totals[:, m, first : first + QUARTER]
+            nc.vector.tensor_tensor(out=total, in0=acc, in1=parent[m, h][:, c : c + QUARTER], op=ADD)
+            result = sb.tile([P, QUARTER], F32, name="result%d_%d" % (m, first))
+            relu(result[:], total)
+            nc.sync.dma_start(out=out[out_rows[m], first : first + QUARTER], in_=result[:])
+
         for i in range(2):
             acc = psum.tile([P, QUARTER], F32, name="y_first0_%d" % i)
-            multiply(acc[:], w1_q, w1_rows[0], first_q[i], slice(0, QUARTER))
-            finish(acc[:], 0, i * QUARTER, scalar_relu, nc.sync)
+            multiply(acc[:], w1_q, out_rows[0], first_q[i], slice(0, QUARTER))
+            finish(acc[:], 0, i * QUARTER, scalar_relu)
         acc = psum.tile([P, HALF], F32, name="y_first1")
         for i in range(2):
-            multiply(acc[:, i * QUARTER : (i + 1) * QUARTER], w1_q, w1_rows[1], first_q[i], slice(0, QUARTER))
+            multiply(acc[:, i * QUARTER : (i + 1) * QUARTER], w1_q, out_rows[1], first_q[i], slice(0, QUARTER))
         for c in (0, QUARTER):
-            finish(acc[:, c : c + QUARTER], 1, c, scalar_relu, nc.sync)
+            finish(acc[:, c : c + QUARTER], 1, c, scalar_relu)
         acc = psum.tile([P, HALF], F32, name="y_second0")
-        multiply(acc[:], w1_q, w1_rows[0], second_q, slice(0, HALF))
+        multiply(acc[:], w1_q, out_rows[0], second_q, slice(0, HALF))
         for c in (0, QUARTER):
-            finish(acc[:, c : c + QUARTER], 0, HALF + c, scalar_relu, nc.sync)
-        for i, (relu, queue) in enumerate(((vector_relu, nc.sync), (scalar_relu, nc.sync))):
+            finish(acc[:, c : c + QUARTER], 0, HALF + c, scalar_relu)
+        for i, relu in enumerate((vector_relu, vector_relu)):
             acc = psum.tile([P, QUARTER], F32, name="y_second1_%d" % i)
-            multiply(acc[:], w1_q, w1_rows[1], second_q, slice(i * QUARTER, (i + 1) * QUARTER))
-            finish(acc[:], 1, HALF + i * QUARTER, relu, queue)
+            multiply(acc[:], w1_q, out_rows[1], second_q, slice(i * QUARTER, (i + 1) * QUARTER))
+            finish(acc[:], 1, HALF + i * QUARTER, relu)

@@ -24,8 +24,8 @@ PAR_PIECE = V // 2
 RUN = 4
 
 FIRST_PLANE, MIDDLE_PLANES, LAST_PLANE = 2, (0, 1), 3
-LAST_CUTS = (0, 1024, 2048, 2816, 3584, 4096)
-VECTOR_PIECE = 3
+LAST_CUTS = (0, 1536, 3072, 3840, 4096)
+VECTOR_SHARE = (0, 768, 512, 0)
 
 
 def tile_picked_fpn_relu_e_kernel(tc, xT, sT, w1, w2, offs, par, out):
@@ -41,16 +41,16 @@ def tile_picked_fpn_relu_e_kernel(tc, xT, sT, w1, w2, offs, par, out):
             return raw
 
         def interleave(copy, raw, name):
-            grouped = sb.tile([P, raw.shape[2], PACK], BF16, name=name + "_bf", align_bytes=64)
+            grouped = sb.tile([P, raw.shape[2], PACK], BF16, name=name + "_bf", tag=name + "_bf", align_bytes=64)
             copy(
                 out=grouped[:].rearrange("p (c i) j -> p c j i", i=RUN),
                 in_=raw.rearrange("p j (c i) -> p c j i", i=RUN),
             )
             return grouped[:]
 
-        def quantize(grouped, name):
+        def quantize(grouped, name, codes_tag=None):
             width = grouped.shape[1]
-            codes = sb.tile([P, width], U32, name=name + "_codes", align_bytes=64)
+            codes = sb.tile([P, width], U32, name=name + "_codes", tag=codes_tag or name + "_codes", align_bytes=64)
             scales = sb.tile([P, width], U8, name=name + "_scales", align_bytes=64)
             nc.vector.quantize_mx(
                 out=codes[:].bitcast(FP8X4), scales=scales[:], in_=grouped.rearrange("p c j -> p (c j)")
@@ -73,7 +73,6 @@ def tile_picked_fpn_relu_e_kernel(tc, xT, sT, w1, w2, offs, par, out):
 
         s_raw = load_rows(sT, "s")
         w2_raw = load_rows(w2, "w2")
-        w1_raw = load_rows(w1, "w1")
         par_sb = lists.tile([P, S // LIST_ROWS], U16, name="par_sb")
         nc.sync.dma_start(par_sb[:], par)
         offs_sb = lists.tile([P, S // LIST_ROWS], U16, name="offs_sb")
@@ -85,18 +84,17 @@ def tile_picked_fpn_relu_e_kernel(tc, xT, sT, w1, w2, offs, par, out):
         last_pieces = [slice(first, end) for first, end in zip(LAST_CUTS, LAST_CUTS[1:])]
         for cols in last_pieces:
             nc.sync.dma_start(out=x_plane[LAST_PLANE][:, cols], in_=x_rows[:, LAST_PLANE, cols])
+        w1_raw = load_rows(w1, "w1")
 
         out_rows = [slice(m * P, (m + 1) * P) for m in range(N // P)]
         s_q = quantize(interleave(nc.vector.tensor_copy, s_raw[:], "s"), "s")
         t_sb = []
         for m, rows in enumerate(out_rows):
             w2_q = quantize(interleave(nc.scalar.copy, w2_raw[:, :, rows], "w2_%d" % m), "w2_%d" % m)
-            t_ps = psum.tile([P, V], F32, name="t_ps%d" % m)
+            t_ps = psum.tile([P, V], F32, name="t_ps%d" % m, tag="t_ps%d" % m)
             multiply(t_ps[:], w2_q, slice(0, P), s_q, slice(0, V))
             t_sb.append(sb.tile([P, V], F32, name="t_sb%d" % m))
             nc.scalar.copy(out=t_sb[m][:], in_=t_ps[:])
-
-        w1_q = quantize(interleave(nc.scalar.copy, w1_raw[:], "w1"), "w1")
 
         parent = {}
 
@@ -120,7 +118,7 @@ def tile_picked_fpn_relu_e_kernel(tc, xT, sT, w1, w2, offs, par, out):
             )
 
         fetch_parents(0)
-        picked = [sb.tile([P, HALF, PACK], BF16, name="picked%d" % h, align_bytes=64) for h in range(2)]
+        picked = [sb.tile([P, HALF, PACK], BF16, name="picked%d" % h, tag="picked%d" % h, align_bytes=64) for h in range(2)]
         first_bf = sb.tile([P, T], BF16, name="first_bf")
         nc.scalar.copy(out=first_bf[:], in_=x_plane[FIRST_PLANE][:])
         gather_on_scalar(FIRST_PLANE, first_bf)
@@ -131,17 +129,19 @@ def tile_picked_fpn_relu_e_kernel(tc, xT, sT, w1, w2, offs, par, out):
             for h in (1, 0):
                 gather_on_vector(j, h)
 
-        last_bf = sb.tile([P, T], BF16, name="last_bf", tag="last_bf")
-        for i, cols in enumerate(last_pieces):
-            copy = nc.vector.tensor_copy if i == VECTOR_PIECE else nc.scalar.copy
-            copy(out=last_bf[:, cols], in_=x_plane[LAST_PLANE][:, cols])
+        last_bf = sb.tile([P, T], BF16, name="last_bf")
+        for cols, share in zip(last_pieces, VECTOR_SHARE):
+            cut = cols.stop - share
+            nc.scalar.copy(out=last_bf[:, cols.start : cut], in_=x_plane[LAST_PLANE][:, cols.start : cut])
+            if share:
+                nc.vector.tensor_copy(out=last_bf[:, cut : cols.stop], in_=x_plane[LAST_PLANE][:, cut : cols.stop])
         gather_on_vector(LAST_PLANE, 0)
         gather_on_scalar(LAST_PLANE, last_bf)
 
         first_q = [quantize(picked[0][:, c : c + QUARTER, :], "x0_%d" % c) for c in (0, QUARTER)]
-        second_q = quantize(picked[1][:], "x1")
-
-        totals = sb.tile([P, N // P, S], F32, name="totals", tag="last_bf")
+        w1_q = [quantize(interleave(nc.vector.tensor_copy, w1_raw[:, :, out_rows[0]], "w1_0"), "w1_0")]
+        second_q = quantize(picked[1][:], "x1", codes_tag="w1_0_bf")
+        w1_q.append(quantize(interleave(nc.scalar.copy, w1_raw[:, :, out_rows[1]], "w1_1"), "w1_1", codes_tag="picked1"))
 
         def scalar_relu(result, total):
             nc.scalar.activation(out=result, in_=total, func=RELU)
@@ -149,28 +149,25 @@ def tile_picked_fpn_relu_e_kernel(tc, xT, sT, w1, w2, offs, par, out):
         def vector_relu(result, total):
             nc.vector.tensor_scalar_max(out=result, in0=total, scalar1=0.0)
 
-        def finish(acc, m, first, relu):
+        def finish(m, first, count, relu):
             h, c = divmod(first, HALF)
-            total = totals[:, m, first : first + QUARTER]
-            nc.vector.tensor_tensor(out=total, in0=acc, in1=parent[m, h][:, c : c + QUARTER], op=ADD)
-            result = sb.tile([P, QUARTER], F32, name="result%d_%d" % (m, first))
-            relu(result[:], total)
-            nc.sync.dma_start(out=out[out_rows[m], first : first + QUARTER], in_=result[:])
+            acc = psum.tile([P, count], F32, name="y%d_%d" % (m, first), tag="t_ps%d" % (first // QUARTER) if m == 0 and h == 0 else "y%d_%d" % (m, first))
+            if h == 0:
+                for q in range(c, c + count, QUARTER):
+                    multiply(acc[:, q - c : q - c + QUARTER], w1_q[m], slice(0, P), first_q[q // QUARTER], slice(0, QUARTER))
+            else:
+                multiply(acc[:], w1_q[m], slice(0, P), second_q, slice(c, c + count))
+            total = sb.tile([P, count], F32, name="total%d_%d" % (m, first))
+            nc.vector.tensor_tensor(out=total[:], in0=acc[:], in1=parent[m, h][:, c : c + count], op=ADD)
+            result = sb.tile([P, count], F32, name="result%d_%d" % (m, first))
+            relu(result[:], total[:])
+            nc.sync.dma_start(out=out[out_rows[m], first : first + count], in_=result[:])
 
-        for i in range(2):
-            acc = psum.tile([P, QUARTER], F32, name="y_first0_%d" % i)
-            multiply(acc[:], w1_q, out_rows[0], first_q[i], slice(0, QUARTER))
-            finish(acc[:], 0, i * QUARTER, scalar_relu)
-        acc = psum.tile([P, HALF], F32, name="y_first1")
-        for i in range(2):
-            multiply(acc[:, i * QUARTER : (i + 1) * QUARTER], w1_q, out_rows[1], first_q[i], slice(0, QUARTER))
-        for c in (0, QUARTER):
-            finish(acc[:, c : c + QUARTER], 1, c, scalar_relu)
-        acc = psum.tile([P, HALF], F32, name="y_second0")
-        multiply(acc[:], w1_q, out_rows[0], second_q, slice(0, HALF))
-        for c in (0, QUARTER):
-            finish(acc[:, c : c + QUARTER], 0, HALF + c, scalar_relu)
-        for i, relu in enumerate((vector_relu, vector_relu)):
-            acc = psum.tile([P, QUARTER], F32, name="y_second1_%d" % i)
-            multiply(acc[:], w1_q, out_rows[1], second_q, slice(i * QUARTER, (i + 1) * QUARTER))
-            finish(acc[:], 1, HALF + i * QUARTER, relu)
+        finish(0, 0, QUARTER, scalar_relu)
+        finish(0, QUARTER, QUARTER, scalar_relu)
+        finish(0, HALF, QUARTER, scalar_relu)
+        finish(0, HALF + QUARTER, QUARTER, scalar_relu)
+        finish(1, 0, QUARTER, scalar_relu)
+        finish(1, QUARTER, QUARTER, scalar_relu)
+        finish(1, HALF, QUARTER, vector_relu)
+        finish(1, HALF + QUARTER, QUARTER, vector_relu)

@@ -24,8 +24,8 @@ PAR_PIECE = V // 2
 RUN = 4
 
 FIRST_PLANE, MIDDLE_PLANES, LAST_PLANE = 2, (0, 1), 3
-LAST_CUTS = (0, 1536, 3072, 3840, 4096)
-VECTOR_SHARE = (0, 768, 512, 0)
+LAST_CUTS = (0, 1280, 2560, 3584, 3840, 4096)
+VECTOR_SHARE = (0, 320, 768, 0, 0)
 
 
 def tile_picked_fpn_relu_e_kernel(tc, xT, sT, w1, w2, offs, par, out):
@@ -36,7 +36,7 @@ def tile_picked_fpn_relu_e_kernel(tc, xT, sT, w1, w2, offs, par, out):
         psum = ctx.enter_context(tc.psum_pool(name="psum", bufs=1))
 
         def load_rows(src, name):
-            raw = sb.tile([P, PACK, src.shape[1]], F32, name=name + "_raw")
+            raw = sb.tile([P, PACK, src.shape[1]], F32, name=name + "_raw", tag=name + "_raw", align_bytes=64)
             nc.sync.dma_start(out=raw[:], in_=src.rearrange("(p j) c -> p j c", j=PACK))
             return raw
 
@@ -48,12 +48,13 @@ def tile_picked_fpn_relu_e_kernel(tc, xT, sT, w1, w2, offs, par, out):
             )
             return grouped[:]
 
-        def quantize(grouped, name, codes_tag=None):
+        def quantize(grouped, name, codes=None):
             width = grouped.shape[1]
-            codes = sb.tile([P, width], U32, name=name + "_codes", tag=codes_tag or name + "_codes", align_bytes=64)
+            if codes is None:
+                codes = sb.tile([P, width], U32, name=name + "_codes", align_bytes=64)[:]
             scales = sb.tile([P, width], U8, name=name + "_scales", align_bytes=64)
             nc.vector.quantize_mx(
-                out=codes[:].bitcast(FP8X4), scales=scales[:], in_=grouped.rearrange("p c j -> p (c j)")
+                out=codes.bitcast(FP8X4), scales=scales[:], in_=grouped.rearrange("p c j -> p (c j)")
             )
             return codes, scales
 
@@ -84,7 +85,7 @@ def tile_picked_fpn_relu_e_kernel(tc, xT, sT, w1, w2, offs, par, out):
         last_pieces = [slice(first, end) for first, end in zip(LAST_CUTS, LAST_CUTS[1:])]
         for cols in last_pieces:
             nc.sync.dma_start(out=x_plane[LAST_PLANE][:, cols], in_=x_rows[:, LAST_PLANE, cols])
-        w1_raw = load_rows(w1, "w1")
+        w1_raw = [load_rows(w1[:, m * P : (m + 1) * P], "w1_%d" % m) for m in range(N // P)]
 
         out_rows = [slice(m * P, (m + 1) * P) for m in range(N // P)]
         s_q = quantize(interleave(nc.vector.tensor_copy, s_raw[:], "s"), "s")
@@ -138,10 +139,13 @@ def tile_picked_fpn_relu_e_kernel(tc, xT, sT, w1, w2, offs, par, out):
         gather_on_vector(LAST_PLANE, 0)
         gather_on_scalar(LAST_PLANE, last_bf)
 
-        first_q = [quantize(picked[0][:, c : c + QUARTER, :], "x0_%d" % c) for c in (0, QUARTER)]
-        w1_q = [quantize(interleave(nc.vector.tensor_copy, w1_raw[:, :, out_rows[0]], "w1_0"), "w1_0")]
-        second_q = quantize(picked[1][:], "x1", codes_tag="w1_0_bf")
-        w1_q.append(quantize(interleave(nc.scalar.copy, w1_raw[:, :, out_rows[1]], "w1_1"), "w1_1", codes_tag="picked1"))
+        w1_first = interleave(nc.vector.tensor_copy, w1_raw[0][:], "w1_0")
+        cell_codes = sb.tile([P, S], U32, name="cell_codes", tag="w1_0_raw", align_bytes=64)
+        first_q = [quantize(picked[0][:, :QUARTER, :], "x0_0", cell_codes[:, :QUARTER])]
+        w1_q = [quantize(w1_first, "w1_0")]
+        first_q.append(quantize(picked[0][:, QUARTER:, :], "x0_1", cell_codes[:, QUARTER:HALF]))
+        second_q = quantize(picked[1][:], "x1", cell_codes[:, HALF:])
+        w1_q.append(quantize(interleave(nc.scalar.copy, w1_raw[1][:], "w1_1"), "w1_1"))
 
         def scalar_relu(result, total):
             nc.scalar.activation(out=result, in_=total, func=RELU)

@@ -24,8 +24,8 @@ PAR_PIECE = V // 2
 RUN = 4
 
 FIRST_PLANE, MIDDLE_PLANES, LAST_PLANE = 2, (0, 1), 3
-LAST_CUTS = (0, 1280, 2560, 3584, 3840, 4096)
-VECTOR_SHARE = (0, 320, 768, 0, 0)
+LAST_CUTS = (0, 1536, 2816, 3584, 4096)
+VECTOR_SHARE = (0, 640, 512, 0)
 
 
 def tile_picked_fpn_relu_e_kernel(tc, xT, sT, w1, w2, offs, par, out):
@@ -144,7 +144,10 @@ def tile_picked_fpn_relu_e_kernel(tc, xT, sT, w1, w2, offs, par, out):
         first_q = [quantize(picked[0][:, :QUARTER, :], "x0_0", cell_codes[:, :QUARTER])]
         w1_q = [quantize(w1_first, "w1_0")]
         first_q.append(quantize(picked[0][:, QUARTER:, :], "x0_1", cell_codes[:, QUARTER:HALF]))
-        second_q = quantize(picked[1][:], "x1", cell_codes[:, HALF:])
+        for c in (0, QUARTER):
+            first_q.append(
+                quantize(picked[1][:, c : c + QUARTER, :], "x1_%d" % c, cell_codes[:, HALF + c : HALF + c + QUARTER])
+            )
         w1_q.append(quantize(interleave(nc.scalar.copy, w1_raw[1][:], "w1_1"), "w1_1"))
 
         def scalar_relu(result, total):
@@ -156,11 +159,7 @@ def tile_picked_fpn_relu_e_kernel(tc, xT, sT, w1, w2, offs, par, out):
         def finish(m, first, count, relu):
             h, c = divmod(first, HALF)
             acc = psum.tile([P, count], F32, name="y%d_%d" % (m, first), tag="t_ps%d" % (first // QUARTER) if m == 0 and h == 0 else "y%d_%d" % (m, first))
-            if h == 0:
-                for q in range(c, c + count, QUARTER):
-                    multiply(acc[:, q - c : q - c + QUARTER], w1_q[m], slice(0, P), first_q[q // QUARTER], slice(0, QUARTER))
-            else:
-                multiply(acc[:], w1_q[m], slice(0, P), second_q, slice(c, c + count))
+            multiply(acc[:], w1_q[m], slice(0, P), first_q[first // QUARTER], slice(0, QUARTER))
             total = sb.tile([P, count], F32, name="total%d_%d" % (m, first))
             nc.vector.tensor_tensor(out=total[:], in0=acc[:], in1=parent[m, h][:, c : c + count], op=ADD)
             result = sb.tile([P, count], F32, name="result%d_%d" % (m, first))

@@ -20,12 +20,12 @@ PACK = 4
 LIST_ROWS = 16
 HALF = S // 2
 QUARTER = S // 4
-PAR_PIECE = V // 2
 RUN = 4
 
-FIRST_PLANE, MIDDLE_PLANES, LAST_PLANE = 2, (0, 1), 3
-LAST_CUTS = (0, 1536, 2816, 3584, 4096)
-VECTOR_SHARE = (0, 640, 512, 0)
+SHARED_PLANE, PAIRED_PLANE, MIDDLE_PLANE, LAST_PLANE = 2, 1, 0, 3
+SHARED_CUT = 3072
+LAST_CUTS = (0, 2560, 3584, 4096)
+VECTOR_SHARE = (1280, 768, 0)
 
 
 def tile_picked_fpn_relu_e_kernel(tc, xT, sT, w1, w2, offs, par, out):
@@ -79,9 +79,12 @@ def tile_picked_fpn_relu_e_kernel(tc, xT, sT, w1, w2, offs, par, out):
         offs_sb = lists.tile([P, S // LIST_ROWS], U16, name="offs_sb")
         nc.sync.dma_start(offs_sb[:], offs)
         x_rows = xT.rearrange("(p j) t -> p j t", j=PACK)
-        x_plane = [sb.tile([P, T], F32, name="x_plane%d" % j) for j in range(PACK)]
-        for j in (FIRST_PLANE, *MIDDLE_PLANES):
-            nc.sync.dma_start(out=x_plane[j][:], in_=x_rows[:, j, :])
+        x_pair = sb.tile([P, 2, T], F32, name="x_pair")
+        nc.sync.dma_start(out=x_pair[:], in_=x_rows[:, PAIRED_PLANE : SHARED_PLANE + 1, :])
+        x_plane = {PAIRED_PLANE: x_pair[:, 0, :], SHARED_PLANE: x_pair[:, 1, :]}
+        for j in (MIDDLE_PLANE, LAST_PLANE):
+            x_plane[j] = sb.tile([P, T], F32, name="x_plane%d" % j)[:]
+        nc.sync.dma_start(out=x_plane[MIDDLE_PLANE], in_=x_rows[:, MIDDLE_PLANE, :])
         last_pieces = [slice(first, end) for first, end in zip(LAST_CUTS, LAST_CUTS[1:])]
         for cols in last_pieces:
             nc.sync.dma_start(out=x_plane[LAST_PLANE][:, cols], in_=x_rows[:, LAST_PLANE, cols])
@@ -100,17 +103,16 @@ def tile_picked_fpn_relu_e_kernel(tc, xT, sT, w1, w2, offs, par, out):
         parent = {}
 
         def fetch_parents(m):
-            for h in range(2):
-                parent[m, h] = sb.tile([P, HALF], F32, name="parent%d%d" % (m, h))
-                for c in range(0, HALF, PAR_PIECE):
-                    nc.vector.tensor_copy(
-                        out=parent[m, h][:, c : c + PAR_PIECE],
-                        in_=t_sb[m][:].indirect(entries(par_sb, h * HALF + c, PAR_PIECE)),
-                    )
+            for q in range(S // QUARTER):
+                name = "parent%d%d" % (m, q)
+                parent[m, q] = sb.tile([P, QUARTER], F32, name=name, tag=name, align_bytes=64)
+                nc.vector.tensor_copy(
+                    out=parent[m, q][:], in_=t_sb[m][:].indirect(entries(par_sb, q * QUARTER, QUARTER))
+                )
 
         def gather_on_vector(j, h):
             nc.vector.tensor_copy(
-                out=picked[h][:, :, j], in_=x_plane[j][:].indirect(entries(offs_sb, h * HALF, HALF))
+                out=picked[h][:, :, j], in_=x_plane[j].indirect(entries(offs_sb, h * HALF, HALF))
             )
 
         def gather_on_scalar(j, plane_bf):
@@ -121,12 +123,13 @@ def tile_picked_fpn_relu_e_kernel(tc, xT, sT, w1, w2, offs, par, out):
         fetch_parents(0)
         picked = [sb.tile([P, HALF, PACK], BF16, name="picked%d" % h, tag="picked%d" % h, align_bytes=64) for h in range(2)]
         first_bf = sb.tile([P, T], BF16, name="first_bf")
-        nc.scalar.copy(out=first_bf[:], in_=x_plane[FIRST_PLANE][:])
-        gather_on_scalar(FIRST_PLANE, first_bf)
-        gather_on_vector(FIRST_PLANE, 0)
         fetch_parents(1)
+        nc.scalar.copy(out=first_bf[:, :SHARED_CUT], in_=x_plane[SHARED_PLANE][:, :SHARED_CUT])
+        nc.vector.tensor_copy(out=first_bf[:, SHARED_CUT:], in_=x_plane[SHARED_PLANE][:, SHARED_CUT:])
+        gather_on_scalar(SHARED_PLANE, first_bf)
+        gather_on_vector(SHARED_PLANE, 0)
 
-        for j in MIDDLE_PLANES:
+        for j in (PAIRED_PLANE, MIDDLE_PLANE):
             for h in (1, 0):
                 gather_on_vector(j, h)
 
@@ -141,36 +144,31 @@ def tile_picked_fpn_relu_e_kernel(tc, xT, sT, w1, w2, offs, par, out):
 
         w1_first = interleave(nc.vector.tensor_copy, w1_raw[0][:], "w1_0")
         cell_codes = sb.tile([P, S], U32, name="cell_codes", tag="w1_0_raw", align_bytes=64)
-        first_q = [quantize(picked[0][:, :QUARTER, :], "x0_0", cell_codes[:, :QUARTER])]
+
+        def quantize_cells(q, codes):
+            h, c = divmod(q * QUARTER, HALF)
+            return quantize(picked[h][:, c : c + QUARTER, :], "x%d" % q, codes)
+
+        def finish(m, q):
+            bank = "t_ps%d" % q if m == 0 and q < 2 else "y%d_%d" % (m, q)
+            acc = psum.tile([P, QUARTER], F32, name="y%d_%d" % (m, q), tag=bank)
+            multiply(acc[:], w1_q[m], slice(0, P), cells_q[q], slice(0, QUARTER))
+            total = sb.tile([P, QUARTER], F32, name="total%d_%d" % (m, q))
+            nc.vector.tensor_tensor(out=total[:], in0=acc[:], in1=parent[m, q][:], op=ADD)
+            result = sb.tile([P, QUARTER], F32, name="result%d_%d" % (m, q))
+            if m == 1 and q >= 2:
+                nc.vector.tensor_scalar_max(out=result[:], in0=total[:], scalar1=0.0)
+            else:
+                nc.scalar.activation(out=result[:], in_=total[:], func=RELU)
+            nc.sync.dma_start(out=out[out_rows[m], q * QUARTER : (q + 1) * QUARTER], in_=result[:])
+
+        cells_q = [quantize_cells(0, cell_codes[:, :QUARTER])]
         w1_q = [quantize(w1_first, "w1_0")]
-        first_q.append(quantize(picked[0][:, QUARTER:, :], "x0_1", cell_codes[:, QUARTER:HALF]))
-        for c in (0, QUARTER):
-            first_q.append(
-                quantize(picked[1][:, c : c + QUARTER, :], "x1_%d" % c, cell_codes[:, HALF + c : HALF + c + QUARTER])
-            )
-        w1_q.append(quantize(interleave(nc.scalar.copy, w1_raw[1][:], "w1_1"), "w1_1"))
-
-        def scalar_relu(result, total):
-            nc.scalar.activation(out=result, in_=total, func=RELU)
-
-        def vector_relu(result, total):
-            nc.vector.tensor_scalar_max(out=result, in0=total, scalar1=0.0)
-
-        def finish(m, first, count, relu):
-            h, c = divmod(first, HALF)
-            acc = psum.tile([P, count], F32, name="y%d_%d" % (m, first), tag="t_ps%d" % (first // QUARTER) if m == 0 and h == 0 else "y%d_%d" % (m, first))
-            multiply(acc[:], w1_q[m], slice(0, P), first_q[first // QUARTER], slice(0, QUARTER))
-            total = sb.tile([P, count], F32, name="total%d_%d" % (m, first))
-            nc.vector.tensor_tensor(out=total[:], in0=acc[:], in1=parent[m, h][:, c : c + count], op=ADD)
-            result = sb.tile([P, count], F32, name="result%d_%d" % (m, first))
-            relu(result[:], total[:])
-            nc.sync.dma_start(out=out[out_rows[m], first : first + count], in_=result[:])
-
-        finish(0, 0, QUARTER, scalar_relu)
-        finish(0, QUARTER, QUARTER, scalar_relu)
-        finish(0, HALF, QUARTER, scalar_relu)
-        finish(0, HALF + QUARTER, QUARTER, scalar_relu)
-        finish(1, 0, QUARTER, scalar_relu)
-        finish(1, QUARTER, QUARTER, scalar_relu)
-        finish(1, HALF, QUARTER, vector_relu)
-        finish(1, HALF + QUARTER, QUARTER, vector_relu)
+        for q in range(1, S // QUARTER):
+            cells_q.append(quantize_cells(q, cell_codes[:, q * QUARTER : (q + 1) * QUARTER]))
+        w1_second = interleave(nc.scalar.copy, w1_raw[1][:], "w1_1")
+        finish(0, 0)
+        w1_codes = sb.tile([P, P], U32, name="w1_1_codes", tag="picked1", align_bytes=64)
+        w1_q.append(quantize(w1_second, "w1_1", w1_codes[:]))
+        for m, q in ((0, 1), (0, 2), (0, 3), (1, 0), (1, 1), (1, 2), (1, 3)):
+            finish(m, q)

@@ -12,6 +12,7 @@ U16 = mybir.dt.uint16
 U8 = mybir.dt.uint8
 FP8X4 = mybir.dt.float8_e4m3fn_x4
 ADD = mybir.AluOpType.add
+MULT = mybir.AluOpType.mult
 COPY = mybir.ActivationFunctionType.Copy
 RELU = mybir.ActivationFunctionType.Relu
 
@@ -22,10 +23,9 @@ HALF = S // 2
 QUARTER = S // 4
 RUN = 4
 
-SHARED_PLANE, PAIRED_PLANE, MIDDLE_PLANE, LAST_PLANE = 2, 1, 0, 3
-SHARED_CUT = 3072
-LAST_CUTS = (0, 2560, 3584, 4096)
-VECTOR_SHARE = (1280, 768, 0)
+FIRST_PLANE, MIDDLE_PLANES, LAST_PLANE = 2, (0, 1), 3
+LAST_CUTS = (0, 1536, 2816, 3584, 4096)
+VECTOR_SHARE = (0, 640, 512, 0)
 
 
 def tile_picked_fpn_relu_e_kernel(tc, xT, sT, w1, w2, offs, par, out):
@@ -79,12 +79,9 @@ def tile_picked_fpn_relu_e_kernel(tc, xT, sT, w1, w2, offs, par, out):
         offs_sb = lists.tile([P, S // LIST_ROWS], U16, name="offs_sb")
         nc.sync.dma_start(offs_sb[:], offs)
         x_rows = xT.rearrange("(p j) t -> p j t", j=PACK)
-        x_pair = sb.tile([P, 2, T], F32, name="x_pair")
-        nc.sync.dma_start(out=x_pair[:], in_=x_rows[:, PAIRED_PLANE : SHARED_PLANE + 1, :])
-        x_plane = {PAIRED_PLANE: x_pair[:, 0, :], SHARED_PLANE: x_pair[:, 1, :]}
-        for j in (MIDDLE_PLANE, LAST_PLANE):
-            x_plane[j] = sb.tile([P, T], F32, name="x_plane%d" % j)[:]
-        nc.sync.dma_start(out=x_plane[MIDDLE_PLANE], in_=x_rows[:, MIDDLE_PLANE, :])
+        x_plane = [sb.tile([P, T], F32, name="x_plane%d" % j) for j in range(PACK)]
+        for j in (FIRST_PLANE, *MIDDLE_PLANES):
+            nc.sync.dma_start(out=x_plane[j][:], in_=x_rows[:, j, :])
         last_pieces = [slice(first, end) for first, end in zip(LAST_CUTS, LAST_CUTS[1:])]
         for cols in last_pieces:
             nc.sync.dma_start(out=x_plane[LAST_PLANE][:, cols], in_=x_rows[:, LAST_PLANE, cols])
@@ -112,7 +109,7 @@ def tile_picked_fpn_relu_e_kernel(tc, xT, sT, w1, w2, offs, par, out):
 
         def gather_on_vector(j, h):
             nc.vector.tensor_copy(
-                out=picked[h][:, :, j], in_=x_plane[j].indirect(entries(offs_sb, h * HALF, HALF))
+                out=picked[h][:, :, j], in_=x_plane[j][:].indirect(entries(offs_sb, h * HALF, HALF))
             )
 
         def gather_on_scalar(j, plane_bf):
@@ -123,13 +120,12 @@ def tile_picked_fpn_relu_e_kernel(tc, xT, sT, w1, w2, offs, par, out):
         fetch_parents(0)
         picked = [sb.tile([P, HALF, PACK], BF16, name="picked%d" % h, tag="picked%d" % h, align_bytes=64) for h in range(2)]
         first_bf = sb.tile([P, T], BF16, name="first_bf")
+        nc.scalar.copy(out=first_bf[:], in_=x_plane[FIRST_PLANE][:])
+        gather_on_scalar(FIRST_PLANE, first_bf)
+        gather_on_vector(FIRST_PLANE, 0)
         fetch_parents(1)
-        nc.scalar.copy(out=first_bf[:, :SHARED_CUT], in_=x_plane[SHARED_PLANE][:, :SHARED_CUT])
-        nc.vector.tensor_copy(out=first_bf[:, SHARED_CUT:], in_=x_plane[SHARED_PLANE][:, SHARED_CUT:])
-        gather_on_scalar(SHARED_PLANE, first_bf)
-        gather_on_vector(SHARED_PLANE, 0)
 
-        for j in (PAIRED_PLANE, MIDDLE_PLANE):
+        for j in MIDDLE_PLANES:
             for h in (1, 0):
                 gather_on_vector(j, h)
 
@@ -142,7 +138,10 @@ def tile_picked_fpn_relu_e_kernel(tc, xT, sT, w1, w2, offs, par, out):
         gather_on_vector(LAST_PLANE, 0)
         gather_on_scalar(LAST_PLANE, last_bf)
 
-        w1_first = interleave(nc.vector.tensor_copy, w1_raw[0][:], "w1_0")
+        w1_first = sb.tile([P, P, PACK], BF16, name="w1_0_bf", align_bytes=64)
+        nc.gpsimd.tensor_scalar(
+            out=w1_first[:], in0=w1_raw[0][:].rearrange("p j c -> p c j"), scalar1=1.0, scalar2=0.0, op0=MULT, op1=ADD
+        )
         cell_codes = sb.tile([P, S], U32, name="cell_codes", tag="w1_0_raw", align_bytes=64)
 
         def quantize_cells(q, codes):
@@ -162,9 +161,9 @@ def tile_picked_fpn_relu_e_kernel(tc, xT, sT, w1, w2, offs, par, out):
                 nc.scalar.activation(out=result[:], in_=total[:], func=RELU)
             nc.sync.dma_start(out=out[out_rows[m], q * QUARTER : (q + 1) * QUARTER], in_=result[:])
 
-        cells_q = [quantize_cells(0, cell_codes[:, :QUARTER])]
-        w1_q = [quantize(w1_first, "w1_0")]
-        for q in range(1, S // QUARTER):
+        w1_q = [quantize(w1_first[:], "w1_0")]
+        cells_q = []
+        for q in range(S // QUARTER):
             cells_q.append(quantize_cells(q, cell_codes[:, q * QUARTER : (q + 1) * QUARTER]))
         w1_second = interleave(nc.scalar.copy, w1_raw[1][:], "w1_1")
         finish(0, 0)

@@ -24,8 +24,8 @@ QUARTER = S // 4
 RUN = 4
 
 FIRST_PLANE, MIDDLE_PLANES, LAST_PLANE = 2, (0, 1), 3
-LAST_CUTS = (0, 1536, 2816, 3584, 4096)
-VECTOR_SHARE = (0, 640, 512, 0)
+LAST_CUTS = (0, 1792, 3072, 3840, 4096)
+VECTOR_SHARE = (0, 1024, 512, 0)
 
 
 def tile_picked_fpn_relu_e_kernel(tc, xT, sT, w1, w2, offs, par, out):

@@ -148,26 +148,30 @@ def tile_picked_fpn_relu_e_kernel(tc, xT, sT, w1, w2, offs, par, out):
             h, c = divmod(q * QUARTER, HALF)
             return quantize(picked[h][:, c : c + QUARTER, :], "x%d" % q, codes)
 
-        def finish(m, q):
+        def finish(m, q, result):
             bank = "t_ps%d" % q if m == 0 and q < 2 else "y%d_%d" % (m, q)
             acc = psum.tile([P, QUARTER], F32, name="y%d_%d" % (m, q), tag=bank)
             multiply(acc[:], w1_q[m], slice(0, P), cells_q[q], slice(0, QUARTER))
             total = sb.tile([P, QUARTER], F32, name="total%d_%d" % (m, q))
             nc.vector.tensor_tensor(out=total[:], in0=acc[:], in1=parent[m, q][:], op=ADD)
-            result = sb.tile([P, QUARTER], F32, name="result%d_%d" % (m, q))
             if m == 1 and q >= 2:
-                nc.vector.tensor_scalar_max(out=result[:], in0=total[:], scalar1=0.0)
+                nc.vector.tensor_scalar_max(out=result, in0=total[:], scalar1=0.0)
             else:
-                nc.scalar.activation(out=result[:], in_=total[:], func=RELU)
-            nc.sync.dma_start(out=out[out_rows[m], q * QUARTER : (q + 1) * QUARTER], in_=result[:])
+                nc.scalar.activation(out=result, in_=total[:], func=RELU)
+
+        def finish_and_store(m, first, count):
+            result = sb.tile([P, count * QUARTER], F32, name="result%d_%d" % (m, first))
+            for i in range(count):
+                finish(m, first + i, result[:, i * QUARTER : (i + 1) * QUARTER])
+            nc.sync.dma_start(out=out[out_rows[m], first * QUARTER : (first + count) * QUARTER], in_=result[:])
 
         w1_q = [quantize(w1_first[:], "w1_0")]
         cells_q = []
         for q in range(S // QUARTER):
             cells_q.append(quantize_cells(q, cell_codes[:, q * QUARTER : (q + 1) * QUARTER]))
         w1_second = interleave(nc.scalar.copy, w1_raw[1][:], "w1_1")
-        finish(0, 0)
-        w1_codes = sb.tile([P, P], U32, name="w1_1_codes", tag="picked1", align_bytes=64)
-        w1_q.append(quantize(w1_second, "w1_1", w1_codes[:]))
-        for m, q in ((0, 1), (0, 2), (0, 3), (1, 0), (1, 1), (1, 2), (1, 3)):
-            finish(m, q)
+        w1_q.append(quantize(w1_second, "w1_1"))
+        for q in range(S // QUARTER):
+            finish_and_store(0, q, 1)
+        finish_and_store(1, 0, 2)
+        finish_and_store(1, 2, 2)

@@ -24,8 +24,9 @@ QUARTER = S // 4
 RUN = 4
 
 FIRST_PLANE, MIDDLE_PLANES, LAST_PLANE = 2, (0, 1), 3
-LAST_CUTS = (0, 1792, 3072, 3840, 4096)
-VECTOR_SHARE = (0, 1024, 512, 0)
+LAST_CUTS = (0, 1920, 3328, 3968, 4096)
+GPSIMD_SHARE = (640, 0, 0, 0)
+VECTOR_SHARE = (0, 896, 448, 0)
 
 
 def tile_picked_fpn_relu_e_kernel(tc, xT, sT, w1, w2, offs, par, out):
@@ -130,11 +131,16 @@ def tile_picked_fpn_relu_e_kernel(tc, xT, sT, w1, w2, offs, par, out):
                 gather_on_vector(j, h)
 
         last_bf = sb.tile([P, T], BF16, name="last_bf")
-        for cols, share in zip(last_pieces, VECTOR_SHARE):
-            cut = cols.stop - share
-            nc.scalar.copy(out=last_bf[:, cols.start : cut], in_=x_plane[LAST_PLANE][:, cols.start : cut])
-            if share:
-                nc.vector.tensor_copy(out=last_bf[:, cut : cols.stop], in_=x_plane[LAST_PLANE][:, cut : cols.stop])
+        last = x_plane[LAST_PLANE]
+        for cols, g_share, v_share in zip(last_pieces, GPSIMD_SHARE, VECTOR_SHARE):
+            g_cut, v_cut = cols.stop - v_share - g_share, cols.stop - v_share
+            nc.scalar.copy(out=last_bf[:, cols.start : g_cut], in_=last[:, cols.start : g_cut])
+            if g_share:
+                nc.gpsimd.tensor_scalar(
+                    out=last_bf[:, g_cut:v_cut], in0=last[:, g_cut:v_cut], scalar1=1.0, scalar2=0.0, op0=MULT, op1=ADD
+                )
+            if v_share:
+                nc.vector.tensor_copy(out=last_bf[:, v_cut : cols.stop], in_=last[:, v_cut : cols.stop])
         gather_on_vector(LAST_PLANE, 0)
         gather_on_scalar(LAST_PLANE, last_bf)
 

@@ -22,11 +22,8 @@ LIST_ROWS = 16
 HALF = S // 2
 QUARTER = S // 4
 RUN = 4
-
-FIRST_PLANE, MIDDLE_PLANES, LAST_PLANE = 2, (0, 1), 3
-LAST_CUTS = (0, 1920, 3328, 3968, 4096)
-GPSIMD_SHARE = (640, 0, 0, 0)
-VECTOR_SHARE = (0, 896, 448, 0)
+LAST_CUTS = (0, 2816, 3840, 4096)
+VECTOR_SHARE = (2112, 544, 0)
 
 
 def tile_picked_fpn_relu_e_kernel(tc, xT, sT, w1, w2, offs, par, out):
@@ -80,12 +77,16 @@ def tile_picked_fpn_relu_e_kernel(tc, xT, sT, w1, w2, offs, par, out):
         offs_sb = lists.tile([P, S // LIST_ROWS], U16, name="offs_sb")
         nc.sync.dma_start(offs_sb[:], offs)
         x_rows = xT.rearrange("(p j) t -> p j t", j=PACK)
-        x_plane = [sb.tile([P, T], F32, name="x_plane%d" % j) for j in range(PACK)]
-        for j in (FIRST_PLANE, *MIDDLE_PLANES):
-            nc.sync.dma_start(out=x_plane[j][:], in_=x_rows[:, j, :])
+        x_pair = sb.tile([P, 2 * T], F32, name="x_pair")
+        nc.sync.dma_start(out=x_pair[:], in_=xT.rearrange("(p j) t -> p (j t)", j=PACK)[:, : 2 * T])
+        x_plane = [x_pair[:, :T], x_pair[:, T:]]
+        third = sb.tile([P, T], F32, name="x_plane2")
+        nc.sync.dma_start(out=third[:], in_=x_rows[:, 2, :])
+        last = sb.tile([P, T], F32, name="x_plane3")
         last_pieces = [slice(first, end) for first, end in zip(LAST_CUTS, LAST_CUTS[1:])]
         for cols in last_pieces:
-            nc.sync.dma_start(out=x_plane[LAST_PLANE][:, cols], in_=x_rows[:, LAST_PLANE, cols])
+            nc.sync.dma_start(out=last[:, cols], in_=x_rows[:, 3, cols])
+        x_plane.extend([third[:], last[:]])
         w1_raw = [load_rows(w1[:, m * P : (m + 1) * P], "w1_%d" % m) for m in range(N // P)]
 
         out_rows = [slice(m * P, (m + 1) * P) for m in range(N // P)]
@@ -99,8 +100,7 @@ def tile_picked_fpn_relu_e_kernel(tc, xT, sT, w1, w2, offs, par, out):
             nc.scalar.copy(out=t_sb[m][:], in_=t_ps[:])
 
         parent = {}
-
-        def fetch_parents(m):
+        for m in range(N // P):
             for q in range(S // QUARTER):
                 name = "parent%d%d" % (m, q)
                 parent[m, q] = sb.tile([P, QUARTER], F32, name=name, tag=name, align_bytes=64)
@@ -108,41 +108,35 @@ def tile_picked_fpn_relu_e_kernel(tc, xT, sT, w1, w2, offs, par, out):
                     out=parent[m, q][:], in_=t_sb[m][:].indirect(entries(par_sb, q * QUARTER, QUARTER))
                 )
 
-        def gather_on_vector(j, h):
-            nc.vector.tensor_copy(
-                out=picked[h][:, :, j], in_=x_plane[j][:].indirect(entries(offs_sb, h * HALF, HALF))
-            )
-
-        def gather_on_scalar(j, plane_bf):
-            nc.scalar.activation(
-                out=picked[1][:, :, j], in_=plane_bf[:].indirect(entries(offs_sb, HALF, HALF)), func=COPY
-            )
-
-        fetch_parents(0)
         picked = [sb.tile([P, HALF, PACK], BF16, name="picked%d" % h, tag="picked%d" % h, align_bytes=64) for h in range(2)]
-        first_bf = sb.tile([P, T], BF16, name="first_bf")
-        nc.scalar.copy(out=first_bf[:], in_=x_plane[FIRST_PLANE][:])
-        gather_on_scalar(FIRST_PLANE, first_bf)
-        gather_on_vector(FIRST_PLANE, 0)
-        fetch_parents(1)
 
-        for j in MIDDLE_PLANES:
-            for h in (1, 0):
-                gather_on_vector(j, h)
+        def gather_on_vector(j):
+            nc.vector.tensor_copy(out=picked[0][:, :, j], in_=x_plane[j].indirect(entries(offs_sb, 0, HALF)))
+
+        def gather_on_scalar(dense, j, first, count):
+            nc.scalar.activation(out=dense, in_=x_plane[j].indirect(entries(offs_sb, HALF + first, count)), func=COPY)
+
+        pair_dense = sb.tile([P, 2, HALF], F32, name="pair_dense")
+        for j in (0, 1):
+            gather_on_vector(j)
+            gather_on_scalar(pair_dense[:, j, :], j, 0, HALF)
+        nc.vector.tensor_copy(out=picked[1][:, :, 0:2], in_=pair_dense[:].rearrange("p j c -> p c j"))
+
+        third_dense = sb.tile([P, HALF], BF16, name="third_dense")
+        gather_on_vector(2)
+        gather_on_scalar(third_dense[:], 2, 0, HALF)
+        nc.scalar.copy(out=picked[1][:, :, 2], in_=third_dense[:])
 
         last_bf = sb.tile([P, T], BF16, name="last_bf")
-        last = x_plane[LAST_PLANE]
-        for cols, g_share, v_share in zip(last_pieces, GPSIMD_SHARE, VECTOR_SHARE):
-            g_cut, v_cut = cols.stop - v_share - g_share, cols.stop - v_share
-            nc.scalar.copy(out=last_bf[:, cols.start : g_cut], in_=last[:, cols.start : g_cut])
-            if g_share:
-                nc.gpsimd.tensor_scalar(
-                    out=last_bf[:, g_cut:v_cut], in0=last[:, g_cut:v_cut], scalar1=1.0, scalar2=0.0, op0=MULT, op1=ADD
-                )
-            if v_share:
-                nc.vector.tensor_copy(out=last_bf[:, v_cut : cols.stop], in_=last[:, v_cut : cols.stop])
-        gather_on_vector(LAST_PLANE, 0)
-        gather_on_scalar(LAST_PLANE, last_bf)
+        for cols, share in zip(last_pieces, VECTOR_SHARE):
+            cut = cols.stop - share
+            nc.scalar.copy(out=last_bf[:, cols.start : cut], in_=last[:, cols.start : cut])
+            if share:
+                nc.vector.tensor_copy(out=last_bf[:, cut : cols.stop], in_=last[:, cut : cols.stop])
+        gather_on_vector(3)
+        nc.scalar.activation(
+            out=picked[1][:, :, 3], in_=last_bf[:].indirect(entries(offs_sb, HALF, HALF)), func=COPY
+        )
 
         w1_first = sb.tile([P, P, PACK], BF16, name="w1_0_bf", align_bytes=64)
         nc.gpsimd.tensor_scalar(

@@ -22,8 +22,8 @@ LIST_ROWS = 16
 HALF = S // 2
 QUARTER = S // 4
 RUN = 4
-LAST_CUTS = (0, 2816, 3840, 4096)
-VECTOR_SHARE = (2112, 544, 0)
+LAST_CUTS = (0, 2880, 3840, 4096)
+VECTOR_SHARE = (1920, 576, 0)
 
 
 def tile_picked_fpn_relu_e_kernel(tc, xT, sT, w1, w2, offs, par, out):
@@ -125,7 +125,7 @@ def tile_picked_fpn_relu_e_kernel(tc, xT, sT, w1, w2, offs, par, out):
         third_dense = sb.tile([P, HALF], BF16, name="third_dense")
         gather_on_vector(2)
         gather_on_scalar(third_dense[:], 2, 0, HALF)
-        nc.scalar.copy(out=picked[1][:, :, 2], in_=third_dense[:])
+        nc.vector.tensor_copy(out=picked[1][:, :, 2], in_=third_dense[:])
 
         last_bf = sb.tile([P, T], BF16, name="last_bf")
         for cols, share in zip(last_pieces, VECTOR_SHARE):

@@ -22,8 +22,6 @@ LIST_ROWS = 16
 HALF = S // 2
 QUARTER = S // 4
 RUN = 4
-LAST_CUTS = (0, 2880, 3840, 4096)
-VECTOR_SHARE = (1920, 576, 0)
 
 
 def tile_picked_fpn_relu_e_kernel(tc, xT, sT, w1, w2, offs, par, out):
@@ -83,9 +81,7 @@ def tile_picked_fpn_relu_e_kernel(tc, xT, sT, w1, w2, offs, par, out):
         third = sb.tile([P, T], F32, name="x_plane2")
         nc.sync.dma_start(out=third[:], in_=x_rows[:, 2, :])
         last = sb.tile([P, T], F32, name="x_plane3")
-        last_pieces = [slice(first, end) for first, end in zip(LAST_CUTS, LAST_CUTS[1:])]
-        for cols in last_pieces:
-            nc.sync.dma_start(out=last[:, cols], in_=x_rows[:, 3, cols])
+        nc.sync.dma_start(out=last[:], in_=x_rows[:, 3, :])
         x_plane.extend([third[:], last[:]])
         w1_raw = [load_rows(w1[:, m * P : (m + 1) * P], "w1_%d" % m) for m in range(N // P)]
 
@@ -122,26 +118,20 @@ def tile_picked_fpn_relu_e_kernel(tc, xT, sT, w1, w2, offs, par, out):
             gather_on_scalar(pair_dense[:, j, :], j, 0, HALF)
         nc.vector.tensor_copy(out=picked[1][:, :, 0:2], in_=pair_dense[:].rearrange("p j c -> p c j"))
 
-        third_dense = sb.tile([P, HALF], BF16, name="third_dense")
+        third_dense = sb.tile([P, HALF], BF16, name="third_dense", tag="dense")
         gather_on_vector(2)
         gather_on_scalar(third_dense[:], 2, 0, HALF)
         nc.vector.tensor_copy(out=picked[1][:, :, 2], in_=third_dense[:])
 
-        last_bf = sb.tile([P, T], BF16, name="last_bf")
-        for cols, share in zip(last_pieces, VECTOR_SHARE):
-            cut = cols.stop - share
-            nc.scalar.copy(out=last_bf[:, cols.start : cut], in_=last[:, cols.start : cut])
-            if share:
-                nc.vector.tensor_copy(out=last_bf[:, cut : cols.stop], in_=last[:, cut : cols.stop])
+        last_dense = sb.tile([P, HALF], BF16, name="last_dense", tag="dense")
         gather_on_vector(3)
-        nc.scalar.activation(
-            out=picked[1][:, :, 3], in_=last_bf[:].indirect(entries(offs_sb, HALF, HALF)), func=COPY
-        )
-
-        w1_first = sb.tile([P, P, PACK], BF16, name="w1_0_bf", align_bytes=64)
+        gather_on_scalar(last_dense[:, :QUARTER], 3, 0, QUARTER)
+        gather_on_scalar(last_dense[:, QUARTER:], 3, QUARTER, QUARTER)
         nc.gpsimd.tensor_scalar(
-            out=w1_first[:], in0=w1_raw[0][:].rearrange("p j c -> p c j"), scalar1=1.0, scalar2=0.0, op0=MULT, op1=ADD
+            out=picked[1][:, :QUARTER, 3], in0=last_dense[:, :QUARTER], scalar1=1.0, scalar2=0.0, op0=MULT, op1=ADD
         )
+        w1_first = interleave(nc.scalar.copy, w1_raw[0][:], "w1_0")
+        nc.scalar.copy(out=picked[1][:, QUARTER:, 3], in_=last_dense[:, QUARTER:])
         cell_codes = sb.tile([P, S], U32, name="cell_codes", tag="w1_0_raw", align_bytes=64)
 
         def quantize_cells(q, codes):
@@ -165,7 +155,7 @@ def tile_picked_fpn_relu_e_kernel(tc, xT, sT, w1, w2, offs, par, out):
                 finish(m, first + i, result[:, i * QUARTER : (i + 1) * QUARTER])
             nc.sync.dma_start(out=out[out_rows[m], first * QUARTER : (first + count) * QUARTER], in_=result[:])
 
-        w1_q = [quantize(w1_first[:], "w1_0")]
+        w1_q = [quantize(w1_first, "w1_0")]
         cells_q = []
         for q in range(S // QUARTER):
             cells_q.append(quantize_cells(q, cell_codes[:, q * QUARTER : (q + 1) * QUARTER]))

@@ -29,6 +29,7 @@ def tile_picked_fpn_relu_e_kernel(tc, xT, sT, w1, w2, offs, par, out):
     with ExitStack() as ctx:
         lists = ctx.enter_context(tc.tile_pool(name="lists", bufs=1))
         sb = ctx.enter_context(tc.tile_pool(name="sb", bufs=1))
+        shared = ctx.enter_context(tc.tile_pool(name="shared", bufs=1))
         psum = ctx.enter_context(tc.psum_pool(name="psum", bufs=1))
 
         def load_rows(src, name):
@@ -118,21 +119,25 @@ def tile_picked_fpn_relu_e_kernel(tc, xT, sT, w1, w2, offs, par, out):
             gather_on_scalar(pair_dense[:, j, :], j, 0, HALF)
         nc.vector.tensor_copy(out=picked[1][:, :, 0:2], in_=pair_dense[:].rearrange("p j c -> p c j"))
 
-        third_dense = sb.tile([P, HALF], BF16, name="third_dense", tag="dense")
+        third_dense = shared.tile([P, HALF], BF16, name="third_dense", offset=256, align_bytes=64)
         gather_on_vector(2)
         gather_on_scalar(third_dense[:], 2, 0, HALF)
         nc.vector.tensor_copy(out=picked[1][:, :, 2], in_=third_dense[:])
 
-        last_dense = sb.tile([P, HALF], BF16, name="last_dense", tag="dense")
+        early_dense = shared.tile([P, QUARTER], BF16, name="early_dense", offset=256, align_bytes=64)
+        late_dense = sb.tile([P, QUARTER], BF16, name="late_dense")
         gather_on_vector(3)
-        gather_on_scalar(last_dense[:, :QUARTER], 3, 0, QUARTER)
-        gather_on_scalar(last_dense[:, QUARTER:], 3, QUARTER, QUARTER)
-        nc.gpsimd.tensor_scalar(
-            out=picked[1][:, :QUARTER, 3], in0=last_dense[:, :QUARTER], scalar1=1.0, scalar2=0.0, op0=MULT, op1=ADD
-        )
+        for first in (0, P):
+            gather_on_scalar(early_dense[:, first : first + P], 3, first, P)
+            nc.gpsimd.tensor_scalar(
+                out=picked[1][:, first : first + P, 3], in0=early_dense[:, first : first + P],
+                scalar1=1.0, scalar2=0.0, op0=MULT, op1=ADD,
+            )
+        gather_on_scalar(late_dense[:], 3, QUARTER, QUARTER)
         w1_first = interleave(nc.scalar.copy, w1_raw[0][:], "w1_0")
-        nc.scalar.copy(out=picked[1][:, QUARTER:, 3], in_=last_dense[:, QUARTER:])
-        cell_codes = sb.tile([P, S], U32, name="cell_codes", tag="w1_0_raw", align_bytes=64)
+        nc.scalar.copy(out=picked[1][:, QUARTER:, 3], in_=late_dense[:])
+        w1_first_codes = shared.tile([P, P], U32, name="w1_first_codes", offset=0, align_bytes=64)
+        cell_codes = shared.tile([P, S], U32, name="cell_codes", offset=512, align_bytes=64)
 
         def quantize_cells(q, codes):
             h, c = divmod(q * QUARTER, HALF)
@@ -155,13 +160,13 @@ def tile_picked_fpn_relu_e_kernel(tc, xT, sT, w1, w2, offs, par, out):
                 finish(m, first + i, result[:, i * QUARTER : (i + 1) * QUARTER])
             nc.sync.dma_start(out=out[out_rows[m], first * QUARTER : (first + count) * QUARTER], in_=result[:])
 
-        w1_q = [quantize(w1_first, "w1_0")]
-        cells_q = []
-        for q in range(S // QUARTER):
-            cells_q.append(quantize_cells(q, cell_codes[:, q * QUARTER : (q + 1) * QUARTER]))
+        cells_q = {2: quantize_cells(2, cell_codes[:, 2 * QUARTER : 3 * QUARTER])}
+        w1_q = [quantize(w1_first, "w1_0", w1_first_codes[:])]
+        for q in (0, 1, 3):
+            cells_q[q] = quantize_cells(q, cell_codes[:, q * QUARTER : (q + 1) * QUARTER])
         w1_second = interleave(nc.scalar.copy, w1_raw[1][:], "w1_1")
         w1_q.append(quantize(w1_second, "w1_1"))
-        for q in range(S // QUARTER):
+        for q in (2, 0, 1, 3):
             finish_and_store(0, q, 1)
         finish_and_store(1, 0, 2)
         finish_and_store(1, 2, 2)

@@ -136,8 +136,8 @@ def tile_picked_fpn_relu_e_kernel(tc, xT, sT, w1, w2, offs, par, out):
         gather_on_scalar(late_dense[:], 3, QUARTER, QUARTER)
         w1_first = interleave(nc.scalar.copy, w1_raw[0][:], "w1_0")
         nc.scalar.copy(out=picked[1][:, QUARTER:, 3], in_=late_dense[:])
-        w1_first_codes = shared.tile([P, P], U32, name="w1_first_codes", offset=0, align_bytes=64)
-        cell_codes = shared.tile([P, S], U32, name="cell_codes", offset=512, align_bytes=64)
+        early_codes = shared.tile([P, QUARTER], U32, name="early_codes", offset=256, align_bytes=64)
+        cell_codes = sb.tile([P, S - QUARTER], U32, name="cell_codes", tag="w1_0_raw", align_bytes=64)
 
         def quantize_cells(q, codes):
             h, c = divmod(q * QUARTER, HALF)
@@ -160,13 +160,14 @@ def tile_picked_fpn_relu_e_kernel(tc, xT, sT, w1, w2, offs, par, out):
                 finish(m, first + i, result[:, i * QUARTER : (i + 1) * QUARTER])
             nc.sync.dma_start(out=out[out_rows[m], first * QUARTER : (first + count) * QUARTER], in_=result[:])
 
-        cells_q = {2: quantize_cells(2, cell_codes[:, 2 * QUARTER : 3 * QUARTER])}
-        w1_q = [quantize(w1_first, "w1_0", w1_first_codes[:])]
-        for q in (0, 1, 3):
-            cells_q[q] = quantize_cells(q, cell_codes[:, q * QUARTER : (q + 1) * QUARTER])
+        cells_q = {2: quantize_cells(2, early_codes[:])}
+        w1_q = [quantize(w1_first, "w1_0")]
+        for i, q in enumerate((0, 1, 3)):
+            cells_q[q] = quantize_cells(q, cell_codes[:, i * QUARTER : (i + 1) * QUARTER])
         w1_second = interleave(nc.scalar.copy, w1_raw[1][:], "w1_1")
+        finish_and_store(0, 2, 1)
         w1_q.append(quantize(w1_second, "w1_1"))
-        for q in (2, 0, 1, 3):
+        for q in (0, 1, 3):
             finish_and_store(0, q, 1)
         finish_and_store(1, 0, 2)
         finish_and_store(1, 2, 2)

@@ -32,9 +32,9 @@ def tile_picked_fpn_relu_e_kernel(tc, xT, sT, w1, w2, offs, par, out):
         shared = ctx.enter_context(tc.tile_pool(name="shared", bufs=1))
         psum = ctx.enter_context(tc.psum_pool(name="psum", bufs=1))
 
-        def load_rows(src, name):
+        def load_rows(src, name, queue=nc.sync):
             raw = sb.tile([P, PACK, src.shape[1]], F32, name=name + "_raw", tag=name + "_raw", align_bytes=64)
-            nc.sync.dma_start(out=raw[:], in_=src.rearrange("(p j) c -> p j c", j=PACK))
+            queue.dma_start(out=raw[:], in_=src.rearrange("(p j) c -> p j c", j=PACK))
             return raw
 
         def interleave(copy, raw, name):
@@ -69,12 +69,12 @@ def tile_picked_fpn_relu_e_kernel(tc, xT, sT, w1, w2, offs, par, out):
         def entries(list_tile, first, count):
             return list_tile[:, first // LIST_ROWS : (first + count) // LIST_ROWS]
 
-        s_raw = load_rows(sT, "s")
-        w2_raw = load_rows(w2, "w2")
+        s_raw = load_rows(sT, "s", nc.scalar)
         par_sb = lists.tile([P, S // LIST_ROWS], U16, name="par_sb")
         nc.sync.dma_start(par_sb[:], par)
         offs_sb = lists.tile([P, S // LIST_ROWS], U16, name="offs_sb")
         nc.sync.dma_start(offs_sb[:], offs)
+        w2_raw = load_rows(w2, "w2")
         x_rows = xT.rearrange("(p j) t -> p j t", j=PACK)
         x_pair = sb.tile([P, 2 * T], F32, name="x_pair")
         nc.sync.dma_start(out=x_pair[:], in_=xT.rearrange("(p j) t -> p (j t)", j=PACK)[:, : 2 * T])

@@ -12,7 +12,6 @@ U16 = mybir.dt.uint16
 U8 = mybir.dt.uint8
 FP8X4 = mybir.dt.float8_e4m3fn_x4
 ADD = mybir.AluOpType.add
-MULT = mybir.AluOpType.mult
 COPY = mybir.ActivationFunctionType.Copy
 RELU = mybir.ActivationFunctionType.Relu
 
@@ -129,10 +128,7 @@ def tile_picked_fpn_relu_e_kernel(tc, xT, sT, w1, w2, offs, par, out):
         gather_on_vector(3)
         for first in (0, P):
             gather_on_scalar(early_dense[:, first : first + P], 3, first, P)
-            nc.gpsimd.tensor_scalar(
-                out=picked[1][:, first : first + P, 3], in0=early_dense[:, first : first + P],
-                scalar1=1.0, scalar2=0.0, op0=MULT, op1=ADD,
-            )
+            nc.gpsimd.tensor_copy(out=picked[1][:, first : first + P, 3], in_=early_dense[:, first : first + P])
         gather_on_scalar(late_dense[:], 3, QUARTER, QUARTER)
         w1_first = interleave(nc.scalar.copy, w1_raw[0][:], "w1_0")
         nc.scalar.copy(out=picked[1][:, QUARTER:, 3], in_=late_dense[:])

@@ -12,6 +12,7 @@ U16 = mybir.dt.uint16
 U8 = mybir.dt.uint8
 FP8X4 = mybir.dt.float8_e4m3fn_x4
 ADD = mybir.AluOpType.add
+MULT = mybir.AluOpType.mult
 COPY = mybir.ActivationFunctionType.Copy
 RELU = mybir.ActivationFunctionType.Relu
 
@@ -28,7 +29,6 @@ def tile_picked_fpn_relu_e_kernel(tc, xT, sT, w1, w2, offs, par, out):
     with ExitStack() as ctx:
         lists = ctx.enter_context(tc.tile_pool(name="lists", bufs=1))
         sb = ctx.enter_context(tc.tile_pool(name="sb", bufs=1))
-        shared = ctx.enter_context(tc.tile_pool(name="shared", bufs=1))
         psum = ctx.enter_context(tc.psum_pool(name="psum", bufs=1))
 
         def load_rows(src, name, queue=nc.sync):
@@ -104,48 +104,58 @@ def tile_picked_fpn_relu_e_kernel(tc, xT, sT, w1, w2, offs, par, out):
                     out=parent[m, q][:], in_=t_sb[m][:].indirect(entries(par_sb, q * QUARTER, QUARTER))
                 )
 
-        picked = [sb.tile([P, HALF, PACK], BF16, name="picked%d" % h, tag="picked%d" % h, align_bytes=64) for h in range(2)]
+        early = sb.tile([P, HALF, PACK], BF16, name="early", align_bytes=64)
+        late = sb.tile([P, P + HALF + P, PACK], BF16, name="late", align_bytes=64)
+        late_cells = late[:, P : P + HALF, :]
 
         def gather_on_vector(j):
-            nc.vector.tensor_copy(out=picked[0][:, :, j], in_=x_plane[j].indirect(entries(offs_sb, 0, HALF)))
+            nc.vector.tensor_copy(out=early[:, :, j], in_=x_plane[j].indirect(entries(offs_sb, 0, HALF)))
 
-        def gather_on_scalar(dense, j, first, count):
-            nc.scalar.activation(out=dense, in_=x_plane[j].indirect(entries(offs_sb, HALF + first, count)), func=COPY)
+        def gather_on_scalar(result, j, first, count):
+            nc.scalar.activation(out=result, in_=x_plane[j].indirect(entries(offs_sb, HALF + first, count)), func=COPY)
 
         pair_dense = sb.tile([P, 2, HALF], F32, name="pair_dense")
         for j in (0, 1):
             gather_on_vector(j)
             gather_on_scalar(pair_dense[:, j, :], j, 0, HALF)
-        nc.vector.tensor_copy(out=picked[1][:, :, 0:2], in_=pair_dense[:].rearrange("p j c -> p c j"))
-
-        third_dense = shared.tile([P, HALF], BF16, name="third_dense", offset=256, align_bytes=64)
+        nc.vector.tensor_copy(out=late_cells[:, :, 0:2], in_=pair_dense[:].rearrange("p j c -> p c j"))
         gather_on_vector(2)
-        gather_on_scalar(third_dense[:], 2, 0, HALF)
-        nc.vector.tensor_copy(out=picked[1][:, :, 2], in_=third_dense[:])
-
-        early_dense = shared.tile([P, QUARTER], BF16, name="early_dense", offset=256, align_bytes=64)
-        late_dense = sb.tile([P, QUARTER], BF16, name="late_dense")
+        gather_on_scalar(late_cells[:, :, 2], 2, 0, HALF)
         gather_on_vector(3)
-        for first in (0, P):
-            gather_on_scalar(early_dense[:, first : first + P], 3, first, P)
-            nc.gpsimd.tensor_copy(out=picked[1][:, first : first + P, 3], in_=early_dense[:, first : first + P])
-        gather_on_scalar(late_dense[:], 3, QUARTER, QUARTER)
-        w1_first = interleave(nc.scalar.copy, w1_raw[0][:], "w1_0")
-        nc.scalar.copy(out=picked[1][:, QUARTER:, 3], in_=late_dense[:])
-        early_codes = shared.tile([P, QUARTER], U32, name="early_codes", offset=256, align_bytes=64)
-        cell_codes = sb.tile([P, S - QUARTER], U32, name="cell_codes", tag="w1_0_raw", align_bytes=64)
+        for first in (0, QUARTER):
+            gather_on_scalar(late_cells[:, first : first + QUARTER, 3], 3, first, QUARTER)
+        nc.gpsimd.tensor_scalar(
+            out=late[:, :P, :], in0=w1_raw[0][:].rearrange("p j c -> p c j"), scalar1=1.0, scalar2=0.0, op0=MULT, op1=ADD
+        )
+        nc.scalar.copy(
+            out=late[:, P + HALF :, :].rearrange("p (c i) j -> p c j i", i=RUN),
+            in_=w1_raw[1][:].rearrange("p j (c i) -> p c j i", i=RUN),
+        )
 
-        def quantize_cells(q, codes):
-            h, c = divmod(q * QUARTER, HALF)
-            return quantize(picked[h][:, c : c + QUARTER, :], "x%d" % q, codes)
+        late_codes = sb.tile([P, P + HALF + P], U32, name="late_codes", align_bytes=64)
+        late_scales = sb.tile([P, P + HALF + P], U8, name="late_scales", align_bytes=64)
+        early_codes = sb.tile([P, HALF], U32, name="early_codes", tag="w1_0_raw", align_bytes=64)
+        early_scales = sb.tile([P, HALF], U8, name="early_scales", align_bytes=64)
+
+        def quantize_columns(codes, scales, grouped, cols):
+            nc.vector.quantize_mx(
+                out=codes[:, cols].bitcast(FP8X4),
+                scales=scales[:, cols],
+                in_=grouped[:, cols, :].rearrange("p c j -> p (c j)"),
+            )
+
+        late_q = (late_codes, late_scales)
+        early_q = (early_codes, early_scales)
+        w1_cols = [slice(0, P), slice(P + HALF, P + HALF + P)]
+        cells = [(early_q, 0), (early_q, QUARTER), (late_q, P), (late_q, P + QUARTER)]
 
         def finish(m, q, result):
             bank = "t_ps%d" % q if m == 0 and q < 2 else "y%d_%d" % (m, q)
             acc = psum.tile([P, QUARTER], F32, name="y%d_%d" % (m, q), tag=bank)
-            multiply(acc[:], w1_q[m], slice(0, P), cells_q[q], slice(0, QUARTER))
+            multiply(acc[:], late_q, w1_cols[m], cells[q][0], slice(cells[q][1], cells[q][1] + QUARTER))
             total = sb.tile([P, QUARTER], F32, name="total%d_%d" % (m, q))
             nc.vector.tensor_tensor(out=total[:], in0=acc[:], in1=parent[m, q][:], op=ADD)
-            if m == 1 and q >= 2:
+            if m == 1 and q == 1:
                 nc.vector.tensor_scalar_max(out=result, in0=total[:], scalar1=0.0)
             else:
                 nc.scalar.activation(out=result, in_=total[:], func=RELU)
@@ -156,14 +166,10 @@ def tile_picked_fpn_relu_e_kernel(tc, xT, sT, w1, w2, offs, par, out):
                 finish(m, first + i, result[:, i * QUARTER : (i + 1) * QUARTER])
             nc.sync.dma_start(out=out[out_rows[m], first * QUARTER : (first + count) * QUARTER], in_=result[:])
 
-        cells_q = {2: quantize_cells(2, early_codes[:])}
-        w1_q = [quantize(w1_first, "w1_0")]
-        for i, q in enumerate((0, 1, 3)):
-            cells_q[q] = quantize_cells(q, cell_codes[:, i * QUARTER : (i + 1) * QUARTER])
-        w1_second = interleave(nc.scalar.copy, w1_raw[1][:], "w1_1")
-        finish_and_store(0, 2, 1)
-        w1_q.append(quantize(w1_second, "w1_1"))
-        for q in (0, 1, 3):
+        quantize_columns(late_codes, late_scales, late, slice(0, P + QUARTER))
+        quantize_columns(early_codes, early_scales, early, slice(0, HALF))
+        quantize_columns(late_codes, late_scales, late, slice(P + QUARTER, P + HALF + P))
+        for q in (2, 0, 1, 3):
             finish_and_store(0, q, 1)
-        finish_and_store(1, 0, 2)
         finish_and_store(1, 2, 2)
+        finish_and_store(1, 0, 2)

@@ -83,7 +83,13 @@ def tile_picked_fpn_relu_e_kernel(tc, xT, sT, w1, w2, offs, par, out):
         last = sb.tile([P, T], F32, name="x_plane3")
         nc.sync.dma_start(out=last[:], in_=x_rows[:, 3, :])
         x_plane.extend([third[:], last[:]])
-        w1_raw = [load_rows(w1[:, m * P : (m + 1) * P], "w1_%d" % m) for m in range(N // P)]
+        w1_rows = w1.rearrange("(p j) c -> p j c", j=PACK)
+        w1_pair = []
+        for u in range(2):
+            name = "w1_pair%d" % u
+            w1_pair.append(sb.tile([P, 2, P], F32, name=name, tag=name, align_bytes=64))
+            nc.sync.dma_start(out=w1_pair[u][:], in_=w1_rows[:, 2 * u : 2 * u + 2, :P])
+        w1_second = load_rows(w1[:, P:], "w1_1")
 
         out_rows = [slice(m * P, (m + 1) * P) for m in range(N // P)]
         s_q = quantize(interleave(nc.vector.tensor_copy, s_raw[:], "s"), "s")
@@ -124,17 +130,23 @@ def tile_picked_fpn_relu_e_kernel(tc, xT, sT, w1, w2, offs, par, out):
         gather_on_vector(3)
         for first in (0, QUARTER):
             gather_on_scalar(late_cells[:, first : first + QUARTER, 3], 3, first, QUARTER)
-        nc.gpsimd.tensor_scalar(
-            out=late[:, :P, :], in0=w1_raw[0][:].rearrange("p j c -> p c j"), scalar1=1.0, scalar2=0.0, op0=MULT, op1=ADD
-        )
+        for u in range(2):
+            nc.gpsimd.tensor_scalar(
+                out=late[:, :P, 2 * u : 2 * u + 2],
+                in0=w1_pair[u][:].rearrange("p j c -> p c j"),
+                scalar1=1.0,
+                scalar2=0.0,
+                op0=MULT,
+                op1=ADD,
+            )
         nc.scalar.copy(
             out=late[:, P + HALF :, :].rearrange("p (c i) j -> p c j i", i=RUN),
-            in_=w1_raw[1][:].rearrange("p j (c i) -> p c j i", i=RUN),
+            in_=w1_second[:].rearrange("p j (c i) -> p c j i", i=RUN),
         )
 
         late_codes = sb.tile([P, P + HALF + P], U32, name="late_codes", align_bytes=64)
         late_scales = sb.tile([P, P + HALF + P], U8, name="late_scales", align_bytes=64)
-        early_codes = sb.tile([P, HALF], U32, name="early_codes", tag="w1_0_raw", align_bytes=64)
+        early_codes = sb.tile([P, HALF], U32, name="early_codes", tag="w1_pair1", align_bytes=64)
         early_scales = sb.tile([P, HALF], U8, name="early_scales", align_bytes=64)
 
         def quantize_columns(codes, scales, grouped, cols):

@@ -179,7 +179,8 @@ def tile_picked_fpn_relu_e_kernel(tc, xT, sT, w1, w2, offs, par, out):
             nc.sync.dma_start(out=out[out_rows[m], first * QUARTER : (first + count) * QUARTER], in_=result[:])
 
         quantize_columns(late_codes, late_scales, late, slice(0, P + QUARTER))
-        quantize_columns(early_codes, early_scales, early, slice(0, HALF))
+        for first in (0, QUARTER):
+            quantize_columns(early_codes, early_scales, early, slice(first, first + QUARTER))
         quantize_columns(late_codes, late_scales, late, slice(P + QUARTER, P + HALF + P))
         for q in (2, 0, 1, 3):
             finish_and_store(0, q, 1)

@@ -29,6 +29,7 @@ def tile_picked_fpn_relu_e_kernel(tc, xT, sT, w1, w2, offs, par, out):
     with ExitStack() as ctx:
         lists = ctx.enter_context(tc.tile_pool(name="lists", bufs=1))
         sb = ctx.enter_context(tc.tile_pool(name="sb", bufs=1))
+        shared = ctx.enter_context(tc.tile_pool(name="shared", bufs=1))
         psum = ctx.enter_context(tc.psum_pool(name="psum", bufs=1))
 
         def load_rows(src, name, queue=nc.sync):
@@ -84,10 +85,11 @@ def tile_picked_fpn_relu_e_kernel(tc, xT, sT, w1, w2, offs, par, out):
         nc.sync.dma_start(out=last[:], in_=x_rows[:, 3, :])
         x_plane.extend([third[:], last[:]])
         w1_rows = w1.rearrange("(p j) c -> p j c", j=PACK)
-        w1_pair = []
+        w1_pair = [
+            sb.tile([P, 2, P], F32, name="w1_pair0", align_bytes=64),
+            shared.tile([P, 2, P], F32, name="w1_pair1", offset=4 * (P + HALF), align_bytes=64),
+        ]
         for u in range(2):
-            name = "w1_pair%d" % u
-            w1_pair.append(sb.tile([P, 2, P], F32, name=name, tag=name, align_bytes=64))
             nc.sync.dma_start(out=w1_pair[u][:], in_=w1_rows[:, 2 * u : 2 * u + 2, :P])
         w1_second = load_rows(w1[:, P:], "w1_1")
 
@@ -144,9 +146,9 @@ def tile_picked_fpn_relu_e_kernel(tc, xT, sT, w1, w2, offs, par, out):
             in_=w1_second[:].rearrange("p j (c i) -> p c j i", i=RUN),
         )
 
-        late_codes = sb.tile([P, P + HALF + P], U32, name="late_codes", align_bytes=64)
+        late_codes = shared.tile([P, P + HALF + P], U32, name="late_codes", offset=0, align_bytes=64)
         late_scales = sb.tile([P, P + HALF + P], U8, name="late_scales", align_bytes=64)
-        early_codes = sb.tile([P, HALF], U32, name="early_codes", tag="w1_pair1", align_bytes=64)
+        early_codes = shared.tile([P, HALF], U32, name="early_codes", offset=4 * (P + HALF + P), align_bytes=64)
         early_scales = sb.tile([P, HALF], U8, name="early_scales", align_bytes=64)
 
         def quantize_columns(codes, scales, grouped, cols):
@@ -179,10 +181,11 @@ def tile_picked_fpn_relu_e_kernel(tc, xT, sT, w1, w2, offs, par, out):
             nc.sync.dma_start(out=out[out_rows[m], first * QUARTER : (first + count) * QUARTER], in_=result[:])
 
         quantize_columns(late_codes, late_scales, late, slice(0, P + QUARTER))
+        quantize_columns(late_codes, late_scales, late, slice(P + QUARTER, P + HALF))
         for first in (0, QUARTER):
             quantize_columns(early_codes, early_scales, early, slice(first, first + QUARTER))
-        quantize_columns(late_codes, late_scales, late, slice(P + QUARTER, P + HALF + P))
-        for q in (2, 0, 1, 3):
+        quantize_columns(late_codes, late_scales, late, w1_cols[1])
+        for q in (2, 3, 0, 1):
             finish_and_store(0, q, 1)
         finish_and_store(1, 2, 2)
         finish_and_store(1, 0, 2)

from contextlib import ExitStack

import concourse.mybir as mybir

K, T, S, V, N = 512, 4096, 1024, 512, 256
FLOPS = 2 * K * N * (S + V)

F32 = mybir.dt.float32
BF16 = mybir.dt.bfloat16
U32 = mybir.dt.uint32
U16 = mybir.dt.uint16
U8 = mybir.dt.uint8
FP8X4 = mybir.dt.float8_e4m3fn_x4
ADD = mybir.AluOpType.add
MULT = mybir.AluOpType.mult
COPY = mybir.ActivationFunctionType.Copy
RELU = mybir.ActivationFunctionType.Relu

P = 128
PACK = 4
LIST_ROWS = 16
HALF = S // 2
QUARTER = S // 4
RUN = 4


def tile_picked_fpn_relu_e_kernel(tc, xT, sT, w1, w2, offs, par, out):
    nc = tc.nc
    with ExitStack() as ctx:
        lists = ctx.enter_context(tc.tile_pool(name="lists", bufs=1))
        sb = ctx.enter_context(tc.tile_pool(name="sb", bufs=1))
        shared = ctx.enter_context(tc.tile_pool(name="shared", bufs=1))
        psum = ctx.enter_context(tc.psum_pool(name="psum", bufs=1))

        def load_rows(src, name, queue=nc.sync):
            raw = sb.tile([P, PACK, src.shape[1]], F32, name=name + "_raw", tag=name + "_raw", align_bytes=64)
            queue.dma_start(out=raw[:], in_=src.rearrange("(p j) c -> p j c", j=PACK))
            return raw

        def interleave(copy, raw, name):
            grouped = sb.tile([P, raw.shape[2], PACK], BF16, name=name + "_bf", tag=name + "_bf", align_bytes=64)
            copy(
                out=grouped[:].rearrange("p (c i) j -> p c j i", i=RUN),
                in_=raw.rearrange("p j (c i) -> p c j i", i=RUN),
            )
            return grouped[:]

        def quantize(grouped, name, codes=None):
            width = grouped.shape[1]
            if codes is None:
                codes = sb.tile([P, width], U32, name=name + "_codes", align_bytes=64)[:]
            scales = sb.tile([P, width], U8, name=name + "_scales", align_bytes=64)
            nc.vector.quantize_mx(
                out=codes.bitcast(FP8X4), scales=scales[:], in_=grouped.rearrange("p c j -> p (c j)")
            )
            return codes, scales

        def multiply(acc, weights, rows, cells, cols):
            nc.tensor.matmul_mx(
                out=acc,
                lhsT=weights[0][:, rows].bitcast(FP8X4),
                lhsT_scale=weights[1][:, rows],
                rhs=cells[0][:, cols].bitcast(FP8X4),
                rhs_scale=cells[1][:, cols],
                start=True,
                stop=True,
            )

        def entries(list_tile, first, count):
            return list_tile[:, first // LIST_ROWS : (first + count) // LIST_ROWS]

        s_raw = load_rows(sT, "s", nc.scalar)
        par_sb = lists.tile([P, S // LIST_ROWS], U16, name="par_sb")
        nc.sync.dma_start(par_sb[:], par)
        offs_sb = lists.tile([P, S // LIST_ROWS], U16, name="offs_sb")
        nc.sync.dma_start(offs_sb[:], offs)
        w2_raw = load_rows(w2, "w2")
        x_rows = xT.rearrange("(p j) t -> p j t", j=PACK)
        x_pair = sb.tile([P, 2 * T], F32, name="x_pair")
        nc.sync.dma_start(out=x_pair[:], in_=xT.rearrange("(p j) t -> p (j t)", j=PACK)[:, : 2 * T])
        x_plane = [x_pair[:, :T], x_pair[:, T:]]
        third = sb.tile([P, T], F32, name="x_plane2")
        nc.sync.dma_start(out=third[:], in_=x_rows[:, 2, :])
        last = sb.tile([P, T], F32, name="x_plane3")
        nc.sync.dma_start(out=last[:], in_=x_rows[:, 3, :])
        x_plane.extend([third[:], last[:]])
        w1_rows = w1.rearrange("(p j) c -> p j c", j=PACK)
        w1_pair = [
            sb.tile([P, 2, P], F32, name="w1_pair0", align_bytes=64),
            shared.tile([P, 2, P], F32, name="w1_pair1", offset=4 * (P + HALF), align_bytes=64),
        ]
        for u in range(2):
            nc.sync.dma_start(out=w1_pair[u][:], in_=w1_rows[:, 2 * u : 2 * u + 2, :P])
        w1_second = load_rows(w1[:, P:], "w1_1")

        out_rows = [slice(m * P, (m + 1) * P) for m in range(N // P)]
        s_q = quantize(interleave(nc.vector.tensor_copy, s_raw[:], "s"), "s")
        t_sb = []
        for m, rows in enumerate(out_rows):
            w2_q = quantize(interleave(nc.scalar.copy, w2_raw[:, :, rows], "w2_%d" % m), "w2_%d" % m)
            t_ps = psum.tile([P, V], F32, name="t_ps%d" % m, tag="t_ps%d" % m)
            multiply(t_ps[:], w2_q, slice(0, P), s_q, slice(0, V))
            t_sb.append(sb.tile([P, V], F32, name="t_sb%d" % m))
            nc.scalar.copy(out=t_sb[m][:], in_=t_ps[:])

        parent = {}
        for m in range(N // P):
            for q in range(S // QUARTER):
                name = "parent%d%d" % (m, q)
                parent[m, q] = sb.tile([P, QUARTER], F32, name=name, tag=name, align_bytes=64)
                nc.vector.tensor_copy(
                    out=parent[m, q][:], in_=t_sb[m][:].indirect(entries(par_sb, q * QUARTER, QUARTER))
                )

        early = sb.tile([P, HALF, PACK], BF16, name="early", align_bytes=64)
        late = sb.tile([P, P + HALF + P, PACK], BF16, name="late", align_bytes=64)
        late_cells = late[:, P : P + HALF, :]

        def gather_on_vector(j):
            nc.vector.tensor_copy(out=early[:, :, j], in_=x_plane[j].indirect(entries(offs_sb, 0, HALF)))

        def gather_on_scalar(result, j, first, count):
            nc.scalar.activation(out=result, in_=x_plane[j].indirect(entries(offs_sb, HALF + first, count)), func=COPY)

        pair_dense = sb.tile([P, 2, HALF], F32, name="pair_dense")
        for j in (0, 1):
            gather_on_vector(j)
            gather_on_scalar(pair_dense[:, j, :], j, 0, HALF)
        nc.vector.tensor_copy(out=late_cells[:, :, 0:2], in_=pair_dense[:].rearrange("p j c -> p c j"))
        gather_on_vector(2)
        gather_on_scalar(late_cells[:, :, 2], 2, 0, HALF)
        gather_on_vector(3)
        for first in (0, QUARTER):
            gather_on_scalar(late_cells[:, first : first + QUARTER, 3], 3, first, QUARTER)
        for u in range(2):
            nc.gpsimd.tensor_scalar(
                out=late[:, :P, 2 * u : 2 * u + 2],
                in0=w1_pair[u][:].rearrange("p j c -> p c j"),
                scalar1=1.0,
                scalar2=0.0,
                op0=MULT,
                op1=ADD,
            )
        nc.scalar.copy(
            out=late[:, P + HALF :, :].rearrange("p (c i) j -> p c j i", i=RUN),
            in_=w1_second[:].rearrange("p j (c i) -> p c j i", i=RUN),
        )

        late_codes = shared.tile([P, P + HALF + P], U32, name="late_codes", offset=0, align_bytes=64)
        late_scales = sb.tile([P, P + HALF + P], U8, name="late_scales", align_bytes=64)
        early_codes = shared.tile([P, HALF], U32, name="early_codes", offset=4 * (P + HALF + P), align_bytes=64)
        early_scales = sb.tile([P, HALF], U8, name="early_scales", align_bytes=64)

        def quantize_columns(codes, scales, grouped, cols):
            nc.vector.quantize_mx(
                out=codes[:, cols].bitcast(FP8X4),
                scales=scales[:, cols],
                in_=grouped[:, cols, :].rearrange("p c j -> p (c j)"),
            )

        late_q = (late_codes, late_scales)
        early_q = (early_codes, early_scales)
        w1_cols = [slice(0, P), slice(P + HALF, P + HALF + P)]
        cells = [(early_q, 0), (early_q, QUARTER), (late_q, P), (late_q, P + QUARTER)]

        def finish(m, q, result):
            bank = "t_ps%d" % q if m == 0 and q < 2 else "y%d_%d" % (m, q)
            acc = psum.tile([P, QUARTER], F32, name="y%d_%d" % (m, q), tag=bank)
            multiply(acc[:], late_q, w1_cols[m], cells[q][0], slice(cells[q][1], cells[q][1] + QUARTER))
            total = sb.tile([P, QUARTER], F32, name="total%d_%d" % (m, q))
            nc.vector.tensor_tensor(out=total[:], in0=acc[:], in1=parent[m, q][:], op=ADD)
            if m == 1 and q == 1:
                nc.vector.tensor_scalar_max(out=result, in0=total[:], scalar1=0.0)
            else:
                nc.scalar.activation(out=result, in_=total[:], func=RELU)

        def finish_and_store(m, first, count):
            result = sb.tile([P, count * QUARTER], F32, name="result%d_%d" % (m, first))
            for i in range(count):
                finish(m, first + i, result[:, i * QUARTER : (i + 1) * QUARTER])
            nc.sync.dma_start(out=out[out_rows[m], first * QUARTER : (first + count) * QUARTER], in_=result[:])

        quantize_columns(late_codes, late_scales, late, slice(0, P + QUARTER))
        quantize_columns(late_codes, late_scales, late, slice(P + QUARTER, P + HALF))
        for first in (0, QUARTER):
            quantize_columns(early_codes, early_scales, early, slice(first, first + QUARTER))
        quantize_columns(late_codes, late_scales, late, w1_cols[1])
        for q in (2, 3, 0, 1):
            finish_and_store(0, q, 1)
        finish_and_store(1, 2, 2)
        finish_and_store(1, 0, 2)
